import numpy as np, ml_dtypes
CORES = [2,3,42,43,82,83,122,123]
N = 8
import mx_ref
BF = ml_dtypes.bfloat16
def f(rng, *shape):
    return mx_ref.flush((rng.standard_normal(shape, dtype=np.float32) * np.exp2(rng.integers(-2, 3, shape[:-1] + (1,)))).astype(BF))
def wide(rng, *shape, cols=0):
    v = rng.standard_normal(shape, dtype=np.float32) * np.exp2(rng.integers(-12, 13, shape)).astype(np.float32)
    if cols: v *= np.repeat(np.exp2(rng.integers(-cols, cols + 1, shape[:-2] + (1, shape[-1] // 4))) * (rng.random(shape[:-2] + (1, shape[-1] // 4)) > 0.0625), 4, axis=-1).astype(np.float32)
    return mx_ref.flush(v.astype(BF))
T, CAPP, O = 512, 96, 1
def scores(us, x):
    return mx_ref.matmul(mx_ref.quantize(us), mx_ref.quantize(x))[:8] + np.float32(0.0)
def winners(us, x):
    return np.argmax(np.stack([scores(us[s], x[s]) for s in range(N)]), axis=0)
def fill(rng, n, tot, most):
    n = np.array(n)
    while n.sum() < tot:
        q = rng.integers(0, N)
        if n[q] < most[q]: n[q] += 1
    return rng.permutation(np.repeat(np.arange(N), n))
def deal(rng, full):
    return np.stack([fill(rng, [CAPP if q in full[g] else 0 for q in range(N)], T, [CAPP] * N) for g in range(8)])
def one(rng):
    g, s = rng.integers(0, 8), rng.integers(0, N)
    return deal(rng, [[s] if i == g else [] for i in range(8)])
def heads(rng):
    u, h = np.zeros((8, 16, 128, 4), np.float32), np.arange(8)
    u[h, :, h] = rng.choice([-1.0, 1.0], (8, 16, 4)) * (0.25 + np.abs(rng.standard_normal((8, 16, 4)))) * np.exp2(rng.integers(-2, 3, (8, 16, 1)))
    return np.repeat(u.reshape(1, 128, 512).astype(BF), N, axis=0)
def plant(rng, x, us, wn, big=4, tie=None, zero=None):
    v = np.abs(x.astype(np.float32)).reshape(N, 8, 16, T, 4)
    v[v < 2.0 ** -24] = 0
    h, b = np.arange(8), np.float32(big)
    a = np.sign(us.astype(np.float32)).reshape(8, 16, 128, 4)[h, :, h][:, :, None]
    win = (wn == np.arange(N)[:, None, None])[:, :, None, :, None]
    neg = (rng.random((8, T)) < 0.125)[:, None, :, None]
    c = np.where(rng.random(v.shape, dtype=np.float32) < 0.5, np.float32(-1), np.float32(1))
    t = (np.where(neg, np.where(win, -a, -4 * b * a), np.where(win, b * a, c)) * v).astype(np.float32)
    s = np.stack([scores(us, t[r].reshape(128, 4 * T).astype(BF)) for r in range(N)])
    won = np.take_along_axis(s, wn[None], axis=0)[0]
    lost = np.where(win[:, :, 0, :, 0], -np.inf, s).max(axis=0)
    bad = (~(won - lost > 0.5 * np.abs(won)))[:, None, :, None]
    t = np.where(bad, np.where(win, b * a, -a) * v, t).astype(np.float32)
    if tie is not None:
        best = np.where(win, t, np.float32(0)).sum(axis=0)
        t = np.where(tie[:, None, :, None] & (wn < np.arange(N)[:, None, None])[:, :, None, :, None], best, t)
    if zero is not None: t[:, :, :, zero] = 0
    return t.reshape(N, 128, 4 * T).astype(BF)
def narrow(rng, x, us, wn):
    v, h = x.astype(np.float32).reshape(N, 8, 16, T, 4), np.arange(8)
    u = np.abs(us.astype(np.float32)).reshape(8, 16, 128, 4)[h, :, h]
    i, b = np.unravel_index(u.reshape(8, 64).argmin(axis=1), (16, 4))
    win = wn == np.arange(N)[:, None, None]
    part = np.where(win[:, :, None, :, None], v, np.float32(0)).sum(axis=0)
    p = np.exp2(np.floor(np.log2((u[:, :, None] * np.abs(part)).sum(axis=(1, 3))) - np.log2(u[h, i, b])[:, None]) - 12)
    z = np.stack([np.where(part[g, i[g], :, b[g]] < 0, -p[g], p[g]) for g in range(8)])
    close = np.repeat((rng.permutation(T) < T // 3)[None], 8, axis=0)
    other = (wn + rng.integers(1, N, (8, T))) % N
    hold = ((rng.random((N, 8, T)) < 0.25) | (other == np.arange(N)[:, None, None])) & ~win & close
    held = hold | (win & close)
    t = np.where(held[:, :, None, :, None], part, v).astype(np.float32)
    d = np.where(hold, rng.choice([-0.125, 0.125], (N, 8, T)), 0.0)
    for k in range(2):
        for g in range(8): t[:, g, i[g], :, b[g]] = np.where(held[:, g], z[g] * (1.5 + d[:, g]), t[:, g, i[g], :, b[g]])
        s = np.stack([scores(us, t[r].reshape(128, 4 * T).astype(BF)) for r in range(N)])
        if k == 0: d = np.where(s == np.take_along_axis(s, wn[None], axis=0), 2 * d, d)
    now = np.argmax(s, axis=0)
    for g in range(8):
        for k in range(T):
            n = np.bincount(now[g], minlength=N)
            q = n.argmax()
            if n[q] <= CAPP: break
            j = rng.permutation(np.flatnonzero((now[g] == q) & (wn[g] != q)))[:n[q] - CAPP]
            now[g, j] = wn[g, j]; close[g, j] = False
    return np.where(close[:, None, :, None], t, v).reshape(N, 128, 4 * T).astype(BF)
def draw(rng, wn, **k):
    us = heads(rng)
    return {"x": plant(rng, f(rng, N, 128, 4 * T), us[0], wn, **k), "us": us, "w": f(rng, N, 128, 512 * O)}
def setup_inputs(rng):
    return draw(rng, one(rng))
def setup_inputs_equal(rng):
    e, p = CAPP - 8, rng.permutation(T)
    far = np.stack([fill(rng, [8] + [0] * (N - 1), T - e, [8] + [CAPP] * (N - 1)) for g in range(8)])
    wn = np.concatenate([np.zeros((8, e), int), far], axis=1)[:, p]
    tie = np.repeat(np.concatenate([np.ones(e, bool), np.arange(T - e) % 2 == 0])[None], 8, axis=0)[:, p]
    return draw(rng, wn, tie=tie, zero=(np.arange(T) < 4)[p])
def setup_inputs_full(rng):
    s, k = int(rng.integers(0, N)), T // CAPP
    return draw(rng, deal(rng, [[s] + [q for q in rng.permutation(N).tolist() if q != s][:k - 1] for g in range(8)]))
def setup_inputs_near(rng):
    wn = one(rng)
    d = draw(rng, wn); d["x"] = narrow(rng, d["x"], d["us"][0], wn); return d
def setup_inputs_spread(rng):
    wn, us = one(rng), heads(rng)
    e = np.exp2(rng.integers(-4, 5, (N, 8, 1, T, 1))) * ((rng.random((N, 8, 1, T, 1)) > 0.0625) | (wn == np.arange(N)[:, None, None])[:, :, None, :, None])
    x = wide(rng, N, 128, 4 * T).astype(np.float32).reshape(N, 8, 16, T, 4) * e.astype(np.float32)
    return {"x": plant(rng, x, us[0], wn, big=256), "us": us, "w": f(rng, N, 128, 512 * O)}
def setup_inputs_stretch(rng):
    L = []
    for g in range(8):
        s, a = rng.integers(0, N), rng.choice([0, T - CAPP, rng.integers(0, T - CAPP + 1)])
        far = fill(rng, [0] * N, T - CAPP, [0 if q == s else CAPP for q in range(N)])
        L.append(np.concatenate([far[:a], np.full(CAPP, s), far[a:]]))
    return draw(rng, np.stack(L))
def check_inputs(d):
    b = []
    for k in ("x", "us", "w"):
        v = np.abs(np.asarray(d[k]).astype(np.float32))
        if not ((v == 0) | ((v >= 2.0 ** -30) & (v <= 2.0 ** 30))).all(): b.append(k)
    if b: return b
    u, h = np.array(d["us"]).astype(np.float32), np.arange(8)
    same = (u == u[:1]).all()
    u = u.reshape(N, 8, 16, 128, 4); u[:, h, :, h] = 0
    if not same or (u != 0).any(): b.append("us")
    wn = winners(d["us"], d["x"])
    if max((wn == s).sum(axis=1).max() for s in range(N)) > CAPP: b.append("x")
    return b
def reference(x, us, w):
    wn = winners(us, x)
    M = []
    for s in range(N):
        v = np.where((wn == s)[:, None, :, None], x[s].astype(np.float32).reshape(8, 16, T, 4), np.float32(0))
        M.append(mx_ref.quantize(np.ascontiguousarray(v.reshape(128, 4 * T).astype(BF))))
    y = np.zeros((N, 128, O * T), np.float32)
    for r in range(N):
        for o in range(O):
            W = mx_ref.quantize(np.ascontiguousarray(w[r][:, 512 * o:512 * o + 512]))
            for s in range(N): y[r][:, T * o:T * o + T] += mx_ref.matmul(W, M[s])
    return {"y": y, "wn": np.repeat(wn.astype(np.float32)[None], N, axis=0)}

@@ -1,0 +1,365 @@
+from concourse.bass import DstId, RemoteDMATransfer
+from concourse.mybir import dt, AluOpType, AxisListType, ActivationFunctionType
+
+F4 = "float8_e4m3fn_x4"
+SCRATCH = {
+    "uw": ("sbuf", [128, 64], "bfloat16"),
+    "xs": ("sbuf", [128, 2048], "bfloat16"),
+    "zt": ("sbuf", [128, 560], "bfloat16"),
+    "wz": ("sbuf", [128, 4096], "bfloat16"),
+    "h": ("sbuf", [128, 512], "bfloat16"),
+    "cz": ("sbuf", [128, 140], F4), "pz": ("sbuf", [128, 140], "uint8"),
+    "cx": ("sbuf", [128, 512], F4), "px": ("sbuf", [128, 512], "uint8"),
+    "cw": ("sbuf", [128, 1024], F4), "pw": ("sbuf", [128, 1024], "uint8"),
+    "ca": ("sbuf", [128, 224], F4), "pa": ("sbuf", [128, 224], "uint8"),
+    "cb": ("sbuf", [128, 288], F4), "pb": ("sbuf", [128, 288], "uint8"),
+    "cc": ("sbuf", [128, 288], F4), "pc": ("sbuf", [128, 288], "uint8"),
+    "ia": ("sbuf", [128, 4], "int32"), "ib": ("sbuf", [128, 4], "int32"), "fa": ("sbuf", [128, 4], "float32"),
+    "g8": ("sbuf", [128, 8], "float32"), "v32": ("sbuf", [128, 128], "float32"), "ms": ("sbuf", [128, 128], "float32"),
+    "oz": ("sbuf", [128, 36], "uint16"),
+    "ic": ("sbuf", [128, 32], "float32"), "c1": ("sbuf", [128, 32], "float32"), "c2": ("sbuf", [128, 32], "float32"),
+    "ij": ("sbuf", [128, 512], "float32"), "cj": ("sbuf", [128, 512], "float32"),
+    "k4": ("sbuf", [128, 96], "float32"), "m4": ("sbuf", [128, 96], "float32"), "r4": ("sbuf", [128, 96], "float32"),
+    "i16": ("sbuf", [128, 32], "float32"), "r16": ("sbuf", [128, 32], "float32"),
+    "i256": ("sbuf", [128, 256], "float32"), "r256": ("sbuf", [128, 256], "float32"),
+    "one": ("sbuf", [128, 32], "float32"), "kc": ("sbuf", [128, 8], "float32"),
+    "sm": ("sbuf", [128, 128], "float32"), "s2": ("sbuf", [128, 64], "float32"), "r": ("sbuf", [128, 256], "float32"),
+    "m1": ("sbuf", [128, 128], "float32"), "m2": ("sbuf", [128, 64], "float32"),
+    "e1": ("sbuf", [128, 32], "float32"), "e2": ("sbuf", [128, 32], "float32"), "e3": ("sbuf", [128, 32], "float32"),
+    "e12": ("sbuf", [128, 32], "float32"), "e": ("sbuf", [128, 32], "float32"),
+    "cs": ("sbuf", [128, 32], "float32"), "t1": ("sbuf", [128, 32], "float32"), "t2": ("sbuf", [128, 32], "float32"), "t3": ("sbuf", [128, 32], "float32"),
+    "v1": ("sbuf", [128, 32], "float32"), "v2": ("sbuf", [128, 32], "float32"), "v3": ("sbuf", [128, 32], "float32"),
+    "ow": ("sbuf", [128, 32], "uint16"), "l": ("sbuf", [128, 512], "float32"),
+    "lm": ("sbuf", [128, 96], "float32"), "ls": ("sbuf", [128, 96], "float32"), "og": ("sbuf", [128, 24], "uint16"),
+    "b1": ("sbuf", [128, 128], "float32"), "b2": ("sbuf", [128, 64], "float32"), "b3": ("sbuf", [128, 32], "float32"),
+    "d1": ("sbuf", [128, 64], "float32"), "d2": ("sbuf", [128, 64], "float32"), "d3": ("sbuf", [128, 64], "float32"), "w2": ("sbuf", [128, 64], "float32"),
+    "f1": ("sbuf", [128, 32], "float32"), "f2": ("sbuf", [128, 32], "float32"), "f3": ("sbuf", [128, 32], "float32"), "win": ("sbuf", [128, 32], "float32"),
+    "ee": ("sbuf", [128, 256], "float32"), "ep": ("sbuf", [128, 256], "float32"), "ca1": ("sbuf", [128, 256], "float32"),
+    "tt": ("sbuf", [128, 32], "float32"), "tu": ("sbuf", [128, 32], "float32"), "tv": ("sbuf", [128, 32], "float32"), "tw": ("sbuf", [128, 32], "float32"),
+    "st1": ("sbuf", [128, 8], "float32"), "st2": ("sbuf", [128, 8], "float32"),
+    "u": ("sbuf", [128, 256], "float32"), "uv": ("sbuf", [128, 256], "float32"),
+    "x1": ("sbuf", [128, 128], "float32"), "x2": ("sbuf", [128, 64], "float32"), "ix": ("sbuf", [128, 32], "float32"), "it": ("sbuf", [128, 32], "float32"),
+    "bx": ("sbuf", [128, 256], "float32"), "off": ("sbuf", [128, 256], "uint16"),
+    "ps": ("psum", [128, 4096], "float32"),
+    "p": ("sbuf", [128, 6400], "float32"), "ya": ("sbuf", [128, 512], "float32"),
+}
+SEMAPHORES = ["lu", "lx0", "lx1", "lx2", "lx3", "lw", "gi", "v", "s", "pe", "it1", "it2", "st",
+              "asc", "aa", "ab", "ac", "loc"]
+
+ADD, SUB, MUL, MAX, MIN = AluOpType.add, AluOpType.subtract, AluOpType.mult, AluOpType.max, AluOpType.min
+GE, GT, EQ = AluOpType.is_ge, AluOpType.is_gt, AluOpType.is_equal
+COPY = ActivationFunctionType.Copy
+
+
+def bitrev(s):
+    return (s & 1) * 4 + (s & 2) + (s >> 2)
+
+
+def rank_program(g, core, T, topo):
+    rank = T.rank_of(core)
+    if rank is None:
+        return
+    S = T.sem
+    V, A, P, Y = g.vector, g.scalar, g.tensor, g.sync
+    n = {"v": 0, "s": 0, "pe": 0, "gi": 0, "loc": 0}
+
+    def inc(q, call):
+        n[q] += 1
+        call.then_inc(S[q], 1)
+        return n[q]
+
+    cores = list(T.cores)
+    chips = []
+    for c in cores:
+        if topo.chip(c) not in chips:
+            chips.append(topo.chip(c))
+    on = lambda ch: [c for c in cores if topo.chip(c) == ch]
+    mychip = topo.chip(core)
+    kind = on(mychip).index(core)
+    mate = [c for c in on(mychip) if c != core][0]
+    far = [c for c in cores if topo.chip(c) != mychip]
+    same = [on(ch)[kind] for ch in chips if ch != mychip]
+    slot = lambda frm, to: [ch for ch in chips if ch != topo.chip(to)].index(topo.chip(frm))
+    eng_far = [e for e in topo.engines(core, far[0])]
+    for c in far:
+        eng_far = [e for e in eng_far if e in topo.engines(core, c)]
+    eng_near = [e for e in topo.engines(core, mate) if e not in eng_far][:4]
+    m_far = sum(1 << e for e in eng_far)
+    m_near = sum(1 << e for e in eng_near)
+    did = lambda c: DstId(rid=topo.addr(c)[0], pnc=topo.addr(c)[1])
+
+    def start_of(s):
+        c = cores[s]
+        if c == core:
+            return 0
+        if c == mate:
+            return 128
+        return (224 if on(topo.chip(c)).index(c) == kind else 512) + 96 * slot(c, core)
+
+    def send(transfers):
+        for t in transfers:
+            n["loc"] += t[0]
+        g.remote_dma_fused([t[1] for t in transfers], local_sem=S.loc)
+
+    Y.dma_start(T.uw[:, 0:64], T.us[:, 0:64]).then_inc(S.lu, 16)
+    for k in (0, 2):
+        Y.dma_start(T.xs[:, 512 * k:512 * k + 512], T.x[:, 512 * k:512 * k + 512]).then_inc(S["lx%d" % k], 16)
+    for k in (1, 3):
+        A.dma_start(T.xs[:, 512 * k:512 * k + 512], T.x[:, 512 * k:512 * k + 512]).then_inc(S["lx%d" % k], 16)
+
+    iota = lambda out, pat, base, cm: inc("gi", g.iota(out, pat, base, cm, allow_small_or_imprecise_dtypes=True))
+    g.iota(T.ia[:, 0:1], [[0, 1]], 0, 1).then_inc(S.gi, 1)
+    g.iota(T.ia[:, 1:2], [[0, 1]], 0, 32).then_inc(S.gi, 1)
+    n["gi"] = 2
+    iota(T.g8[:, :], [[4, 8]], 0, 0)
+    k_i0 = n["gi"]
+    iota(T.v32[:, :], [[1, 4], [0, 32]], 0, 0)
+    k_v32 = n["gi"]
+    iota(T.ic[:, :], [[1, 32]], -512, 0)
+    iota(T.k4[:, :], [[0, 24], [1, 4]], 0, 0)
+    iota(T.i16[:, :], [[0, 2], [1, 16]], 0, 0)
+    iota(T.ij[:, :], [[4, 32], [128, 16]], 0, 0)
+    iota(T.i256[:, :], [[0, 8], [1, 32]], 0, 0)
+    k_iall = n["gi"]
+
+    k = inc("v", V.memset(T.oz[:, :], 32))
+    V.wait_ge(S.gi, k_i0)
+    AND = AluOpType.bitwise_and
+    inc("v", V.tensor_scalar(T.ib[:, 0:1], T.ia[:, 0:1], 3, None, AND))
+    inc("v", V.tensor_scalar(T.ib[:, 1:2], T.ia[:, 1:2], 511, None, AND))
+    inc("v", V.tensor_scalar(T.ib[:, 2:3], T.ia[:, 0:1], 12, 2, AND, AluOpType.arith_shift_right))
+    V.wait_ge(S.v, n["v"])
+    inc("v", V.tensor_copy(T.fa[:, 0:3], T.ib[:, 0:3]))
+    V.wait_ge(S.v, n["v"])
+    v_oz = inc("v", V.tensor_scalar(T.oz[:, 3:32:4], T.g8[:, :], T.fa[:, 0:1], None, ADD))
+    v_wz = inc("v", V.memset(T.wz[:, :], 0.0))
+    V.wait_ge(S.gi, k_v32)
+    inc("v", V.tensor_scalar(T.ms[:, :], T.v32[:, :], T.fa[:, 0:1], None, EQ))
+    inc("v", V.memset(T.h[:, 384:512], 0.0))
+
+    A.wait_ge(S.lu, 16)
+    A.wait_ge(S.v, v_oz)
+    s_zt = inc("s", A.activation(T.zt[:, 0:560], T.uw[:, 0:64].indirect(T.oz[:, 0:35]), COPY))
+
+    Y.wait_ge(S.v, v_wz)
+    for q in range(8):
+        Y.dma_start(T.wz[16 * q:16 * q + 16, 512 * q:512 * q + 512], T.w[16 * q:16 * q + 16, :]).then_inc(S.lw, 16)
+
+    V.wait_ge(S.s, s_zt)
+    inc("v", V.quantize_mx(T.cz[:, :], T.pz[:, :], T.zt[:, :]))
+    for q in range(4):
+        V.wait_ge(S["lx%d" % q], 16)
+        kq = inc("v", V.quantize_mx(T.cx[:, 128 * q:128 * q + 128], T.px[:, 128 * q:128 * q + 128], T.xs[:, 512 * q:512 * q + 512]))
+        P.wait_ge(S.v, kq)
+        a = 12 - 4 * q
+        k_sc = inc("pe", P.matmul_mx(T.ps[:, 3584:3712], T.cz[:, a:a + 128], T.pz[:, a:a + 128],
+                                     T.cx[:, 128 * q:128 * q + 128], T.px[:, 128 * q:128 * q + 128], q == 0, q == 3))
+    V.wait_ge(S.pe, k_sc)
+    me = bitrev(rank)
+    own = T.r[:, 32 * me:32 * me + 32]
+    V.wait_ge(S.v, inc("v", V.tensor_tensor(T.sm[:, :], T.ps[:, 3584:3712], T.ms[:, :], MUL)))
+    V.wait_ge(S.v, inc("v", V.tensor_tensor(T.s2[:, :], T.sm[:, 0:64], T.sm[:, 64:128], ADD)))
+    v_own = inc("v", V.tensor_tensor(own, T.s2[:, 0:32], T.s2[:, 32:64], ADD))
+    g.wait_ge(S.v, v_own)
+    send([(len(eng_far), RemoteDMATransfer(dst_ids=[did(c) for c in far], dma_engine_mask=m_far, remote_sem=S.asc,
+                                           srcs=[own], dsts=[own] * len(far), alu_op=0)),
+          (len(eng_near), RemoteDMATransfer(dst_ids=[did(mate)], dma_engine_mask=m_near, remote_sem=S.asc,
+                                            srcs=[own], dsts=[own], alu_op=0))])
+
+    V.wait_ge(S.gi, k_iall)
+    inc("v", V.tensor_scalar(T.c1[:, :], T.ic[:, :], T.fa[:, 0:1] if False else T.fa[:, 1:2], None, ADD))
+    kc1 = n["v"]
+    inc("v", V.tensor_scalar(T.cj[:, :], T.ij[:, :], T.fa[:, 0:1], None, ADD))
+    inc("v", V.tensor_scalar(T.m4[:, :], T.k4[:, :], T.fa[:, 2:3], None, EQ))
+    inc("v", V.tensor_scalar(T.r4[:, :], T.k4[:, :], 1.0, None, MIN))
+    inc("v", V.tensor_scalar(T.r16[:, :], T.i16[:, :], 1.0, None, MIN))
+    inc("v", V.tensor_scalar(T.r256[:, :], T.i256[:, :], 1.0, None, MIN))
+    inc("v", V.memset(T.one[:, :], 1.0))
+    inc("v", V.memset(T.tt[:, :], 0.0))
+    for s in range(8):
+        inc("v", V.memset(T.kc[:, s:s + 1], float(start_of(s) - 1)))
+    V.wait_ge(S.v, kc1)
+    inc("v", V.tensor_scalar(T.c2[:, :], T.c1[:, :], -1.0, -1.0, MUL, ADD))
+    V.wait_ge(S.lw, 128)
+    inc("v", V.quantize_mx(T.cw[:, 0:512], T.pw[:, 0:512], T.wz[:, 0:2048]))
+    v_w = inc("v", V.quantize_mx(T.cw[:, 512:1024], T.pw[:, 512:1024], T.wz[:, 2048:4096]))
+
+    vw = lambda k: V.wait_ge(S.v, k)
+    R = lambda b, q=1: T.r[:, 32 * b:32 * (b + q)]
+    V.wait_ge(S.asc, len(eng_far) * len(far) + len(eng_near))
+    vw(n["v"])
+    sib = lambda bit: GE if not bit else GT
+    lo, hi = me & 3, me & 1
+    k1 = inc("v", V.tensor_tensor(T.m1[:, :], R(0, 4), R(4, 4), MAX))
+    inc("v", V.tensor_tensor(T.e1[:, :], own, R(me ^ 4), sib(me & 4)))
+    vw(k1)
+    k2 = inc("v", V.tensor_tensor(T.m2[:, :], T.m1[:, 0:64], T.m1[:, 64:128], MAX))
+    ke2 = inc("v", V.tensor_tensor(T.e2[:, :], T.m1[:, 32 * lo:32 * lo + 32], T.m1[:, 32 * (lo ^ 2):32 * (lo ^ 2) + 32], sib(me & 2)))
+    vw(k2)
+    k3 = inc("v", V.tensor_tensor(T.e3[:, :], T.m2[:, 32 * hi:32 * hi + 32], T.m2[:, 32 * (hi ^ 1):32 * (hi ^ 1) + 32], sib(me & 1)))
+    vw(ke2)
+    k4 = inc("v", V.tensor_tensor(T.e12[:, :], T.e1[:, :], T.e2[:, :], MUL))
+    vw(k4)
+    ke = inc("v", V.tensor_tensor(T.e[:, :], T.e12[:, :], T.e3[:, :], MUL))
+    vw(ke)
+    kcs = inc("v", V.tensor_tensor_scan(T.cs[:, :], T.one[:, :], T.e[:, :], 0.0, MUL, ADD))
+    kv1 = inc("v", V.tensor_tensor(T.v1[:, :], T.e[:, :], T.c1[:, :], MUL))
+    vw(kcs)
+    kt1 = inc("v", V.transpose(T.t1[:, :], T.cs[:, :]))
+    vw(kv1)
+    kv2 = inc("v", V.tensor_tensor(T.v2[:, :], T.v1[:, :], T.c2[:, :], ADD))
+    vw(kt1)
+    kt2 = inc("v", V.tensor_tensor_scan(T.t2[:, :], T.r16[:, :], T.t1[:, :], 0.0, MUL, ADD))
+    vw(kv2)
+    kv3 = inc("v", V.tensor_tensor(T.v3[:, :], T.v2[:, :], T.cs[:, :], ADD))
+    vw(kt2)
+    kt3 = inc("v", V.transpose(T.t3[:, :], T.t2[:, :]))
+    vw(kt3)
+    k = inc("v", V.tensor_scalar(T.ow[:, :], T.v3[:, :], T.t3[:, 31:32], T.cs[:, 31:32], ADD, SUB))
+    vw(k)
+    k = inc("v", V.tensor_copy(T.l[:, 0:512].indirect(T.ow[:, 0:32]), T.cj[:, :]))
+    vw(k)
+    k = inc("v", V.tensor_tensor(T.lm[:, :], T.l[:, 0:96], T.m4[:, :], MUL))
+    vw(k)
+    k = inc("v", V.tensor_tensor_scan(T.ls[:, :], T.r4[:, :], T.lm[:, :], 0.0, MUL, ADD))
+    vw(k)
+    v_og = inc("v", V.tensor_copy(T.og[:, :], T.ls[:, 3:96:4]))
+    vw(v_og)
+    k = inc("v", V.tensor_copy(T.h[:, 0:192], T.xs[:, 0:2048].indirect(T.og[:, 0:12])))
+    A.wait_ge(S.v, v_og)
+    s_h = inc("s", A.activation(T.h[:, 192:384], T.xs[:, 0:2048].indirect(T.og[:, 12:24]), COPY))
+    vw(k)
+    V.wait_ge(S.s, s_h)
+    v_q = inc("v", V.quantize_mx(T.ca[:, 0:128], T.pa[:, 0:128], T.h[:, :]))
+    g.wait_ge(S.v, v_q)
+    oc, op = T.ca[:, 0:96].bitcast(dt.uint8), T.pa[:, 0:96]
+    for src, to_far, to_near in (
+            (oc, [T.cb[:, 96 * slot(core, c):96 * slot(core, c) + 96].bitcast(dt.uint8) for c in same], T.ca[:, 128:224].bitcast(dt.uint8)),
+            (op, [T.pb[:, 96 * slot(core, c):96 * slot(core, c) + 96] for c in same], T.pa[:, 128:224])):
+        send([(len(eng_far), RemoteDMATransfer(dst_ids=[did(c) for c in same], dma_engine_mask=m_far, remote_sem=S.ab,
+                                               srcs=[src], dsts=to_far, alu_op=0)),
+              (len(eng_near), RemoteDMATransfer(dst_ids=[did(mate)], dma_engine_mask=m_near, remote_sem=S.aa,
+                                                srcs=[src], dsts=[to_near], alu_op=0))])
+    n_aa, n_ab, n_ac = 2 * len(eng_near), 2 * len(eng_far) * len(same), len(eng_far) + len(eng_near)
+    g.wait_ge(S.ab, n_ab)
+    send([(len(eng_far), RemoteDMATransfer(dst_ids=[did(mate)], dma_engine_mask=m_far, remote_sem=S.ac,
+                                           srcs=[T.cb[:, :].bitcast(dt.uint8)], dsts=[T.cc[:, :].bitcast(dt.uint8)], alu_op=0))])
+    send([(len(eng_near), RemoteDMATransfer(dst_ids=[did(mate)], dma_engine_mask=m_near, remote_sem=S.ac,
+                                            srcs=[T.pb[:, :]], dsts=[T.pc[:, :]], alu_op=0))])
+
+    kb1 = inc("v", V.tensor_tensor(T.b1[:, :], R(4, 4), R(0, 4), GT))
+    inc("v", V.tensor_tensor(T.b2[:, :], T.m1[:, 64:128], T.m1[:, 0:64], GT))
+    inc("v", V.tensor_tensor(T.b3[:, :], T.m2[:, 32:64], T.m2[:, 0:32], GT))
+    vw(kb1)
+    k = inc("v", V.tensor_tensor(T.d1[:, :], T.b1[:, 64:128], T.b1[:, 0:64], SUB))
+    vw(k)
+    k = inc("v", V.tensor_scalar(T.d2[:, :], T.d1[:, :], 2.0, None, ADD))
+    vw(k)
+    k = inc("v", V.tensor_tensor(T.d3[:, :], T.d2[:, :], T.b2[:, :], MUL))
+    vw(k)
+    k = inc("v", V.tensor_tensor(T.w2[:, :], T.d3[:, :], T.b1[:, 0:64], ADD))
+    vw(k)
+    k = inc("v", V.tensor_tensor(T.f1[:, :], T.w2[:, 32:64], T.w2[:, 0:32], SUB))
+    vw(k)
+    k = inc("v", V.tensor_scalar(T.f2[:, :], T.f1[:, :], 4.0, None, ADD))
+    vw(k)
+    k = inc("v", V.tensor_tensor(T.f3[:, :], T.f2[:, :], T.b3[:, :], MUL))
+    vw(k)
+    v_win = inc("v", V.tensor_tensor(T.win[:, :], T.f3[:, :], T.w2[:, 0:32], ADD))
+    vw(v_win)
+    for s in range(8):
+        v_ee = inc("v", V.tensor_scalar(T.ee[:, 32 * s:32 * s + 32], T.win[:, :], float(s), None, EQ))
+    A.wait_ge(S.v, v_ee)
+    s_ep = inc("s", A.activation(T.ep[:, :], T.ee[:, :], COPY))
+    vw(v_ee)
+    k = inc("v", V.tensor_tensor_scan(T.ca1[:, :], T.r256[:, :], T.ee[:, :], 0.0, MUL, ADD))
+    vw(k)
+    k = inc("v", V.tensor_copy(T.tt[:, 0:8], T.ca1[:, 31:256:32]))
+    vw(k)
+    k = inc("v", V.transpose(T.tu[:, :], T.tt[:, :]))
+    vw(k)
+    k = inc("v", V.tensor_tensor_scan(T.tv[:, :], T.r16[:, :], T.tu[:, :], 0.0, MUL, ADD))
+    inc("v", V.tensor_tensor(T.st1[:, :], T.kc[:, :], T.tt[:, 0:8], SUB))
+    vw(k)
+    k = inc("v", V.transpose(T.tw[:, :], T.tv[:, :]))
+    vw(k)
+    k = inc("v", V.tensor_tensor(T.st2[:, :], T.st1[:, :], T.tw[:, 0:8], ADD))
+    vw(k)
+    V.wait_ge(S.s, s_ep)
+    k = inc("v", V.tensor_tensor(T.ep[:, 0:256:32], T.ep[:, 0:256:32], T.st2[:, :], ADD))
+    vw(k)
+    k = inc("v", V.tensor_tensor_scan(T.u[:, :], T.r256[:, :], T.ep[:, :], 0.0, MUL, ADD))
+    vw(k)
+    k = inc("v", V.tensor_tensor(T.uv[:, :], T.u[:, :], T.ee[:, :], MUL))
+    vw(k)
+    k = inc("v", V.tensor_tensor(T.x1[:, :], T.uv[:, 0:128], T.uv[:, 128:256], ADD))
+    vw(k)
+    k = inc("v", V.tensor_tensor(T.x2[:, :], T.x1[:, 0:64], T.x1[:, 64:128], ADD))
+    vw(k)
+    k = inc("v", V.tensor_tensor(T.ix[:, :], T.x2[:, 0:32], T.x2[:, 32:64], ADD))
+    vw(k)
+    v_it = inc("v", V.transpose(T.it[:, :], T.ix[:, :]))
+    Y.wait_ge(S.v, v_it)
+    for q in range(4):
+        for b in range(2):
+            Y.dma_start(T.bx[0:16, 128 * b + 32 * q:128 * b + 32 * q + 32], T.it[32 * q + 16 * b:32 * q + 16 * b + 16, :]).then_inc(S.it1, 16)
+    Y.wait_ge(S.it1, 128)
+    for q in range(1, 8):
+        Y.dma_start(T.bx[16 * q:16 * q + 16, :], T.bx[0:16, :]).then_inc(S.it2, 16)
+    Y.dma_start(T.wn[:, :], T.win[:, :]).then_inc(S.st, 16)
+
+    bank = lambda q, w: T.ps[:, 512 * q:512 * q + w]
+    wq = lambda q: (T.cw[:, 128 * q:128 * q + 128], T.pw[:, 128 * q:128 * q + 128])
+    done = [None] * 8
+
+    def product(q, codes, plane, w):
+        if done[q]:
+            P.wait_ge(S[done[q][0]], done[q][1])
+        return inc("pe", P.matmul_mx(bank(q, w), wq(q)[0], wq(q)[1], codes[:, 0:w], plane[:, 0:w], True, True))
+
+    def out_of(q, at, w, k, vec):
+        eng, key = (V, "v") if vec else (A, "s")
+        eng.wait_ge(S.pe, k)
+        dst = T.p[:, 800 * q + at:800 * q + at + w]
+        done[q] = (key, inc(key, V.tensor_copy(dst, bank(q, w)) if vec else A.activation(dst, bank(q, w), COPY)))
+
+    P.wait_ge(S.v, v_q)
+    P.wait_ge(S.aa, n_aa)
+    for q in range(8):
+        out_of(q, 0, 224, product(q, T.ca, T.pa, 224), False)
+    P.wait_ge(S.ab, n_ab)
+    for q in (0, 4, 1, 5, 2, 6, 3, 7):
+        out_of(q, 224, 288, product(q, T.cb, T.pb, 288), q > 3)
+    v_b = n["v"]
+    P.wait_ge(S.ac, n_ac)
+    for q in range(8):
+        out_of(q, 512, 288, product(q, T.cc, T.pc, 288), False)
+
+    V.wait_ge(S.it2, 112)
+    V.wait_ge(S.it1, 128)
+    inc("v", V.tensor_copy(T.off[:, 0:256:2], T.bx[:, 0:128]))
+    inc("v", V.tensor_copy(T.off[:, 1:256:2], T.bx[:, 128:256]))
+    vw(n["v"])
+
+    def pick(q, a, b, last):
+        out = T.ya[:, a:b]
+        src = T.p[:, 800 * q:800 * q + 800].indirect(T.off[:, 32 * q + a // 16:32 * q + b // 16])
+        if last:
+            vw(last)
+        return inc("v", V.tensor_tensor(out, src, out, ADD) if last else V.tensor_copy(out, src))
+
+    last = 0
+    for q in range(6):
+        V.wait_ge(S.s, done[q][1])
+        last = pick(q, 0, 512, last)
+    for a in (0, 256):
+        for q in (6, 7):
+            V.wait_ge(S.s, done[q][1])
+            k = pick(q, a, a + 256, last if q == 6 else k)
+        Y.wait_ge(S.v, k)
+        Y.dma_start(T.y[:, a:a + 256], T.ya[:, a:a + 256]).then_inc(S.st, 16)
+    Y.wait_ge(S.st, 48)
+    g.wait_ge(S.loc, n["loc"])
+    g.wait_ge(S.v, n["v"])
+    g.wait_ge(S.s, n["s"])
+    g.wait_ge(S.pe, n["pe"])

@@ -1,53 +1,25 @@
 from concourse.bass import DstId, RemoteDMATransfer
-from concourse.mybir import dt, AluOpType, AxisListType, ActivationFunctionType
+from concourse.mybir import dt, AluOpType, ActivationFunctionType
 
-F4 = "float8_e4m3fn_x4"
-SCRATCH = {
-    "uw": ("sbuf", [128, 64], "bfloat16"),
-    "xs": ("sbuf", [128, 2048], "bfloat16"),
-    "zt": ("sbuf", [128, 560], "bfloat16"),
-    "wz": ("sbuf", [128, 4096], "bfloat16"),
-    "h": ("sbuf", [128, 512], "bfloat16"),
-    "cz": ("sbuf", [128, 140], F4), "pz": ("sbuf", [128, 140], "uint8"),
-    "cx": ("sbuf", [128, 512], F4), "px": ("sbuf", [128, 512], "uint8"),
-    "cw": ("sbuf", [128, 1024], F4), "pw": ("sbuf", [128, 1024], "uint8"),
-    "ca": ("sbuf", [128, 224], F4), "pa": ("sbuf", [128, 224], "uint8"),
-    "cb": ("sbuf", [128, 288], F4), "pb": ("sbuf", [128, 288], "uint8"),
-    "cc": ("sbuf", [128, 288], F4), "pc": ("sbuf", [128, 288], "uint8"),
-    "ia": ("sbuf", [128, 4], "int32"), "ib": ("sbuf", [128, 4], "int32"), "fa": ("sbuf", [128, 4], "float32"),
-    "g8": ("sbuf", [128, 8], "float32"), "v32": ("sbuf", [128, 128], "float32"), "ms": ("sbuf", [128, 128], "float32"),
-    "oz": ("sbuf", [128, 36], "uint16"),
-    "ic": ("sbuf", [128, 32], "float32"), "c1": ("sbuf", [128, 32], "float32"), "c2": ("sbuf", [128, 32], "float32"),
-    "ij": ("sbuf", [128, 512], "float32"), "cj": ("sbuf", [128, 512], "float32"),
-    "k4": ("sbuf", [128, 96], "float32"), "m4": ("sbuf", [128, 96], "float32"), "r4": ("sbuf", [128, 96], "float32"),
-    "i16": ("sbuf", [128, 32], "float32"), "r16": ("sbuf", [128, 32], "float32"),
-    "i256": ("sbuf", [128, 256], "float32"), "r256": ("sbuf", [128, 256], "float32"),
-    "one": ("sbuf", [128, 32], "float32"), "kc": ("sbuf", [128, 8], "float32"),
-    "sm": ("sbuf", [128, 128], "float32"), "s2": ("sbuf", [128, 64], "float32"), "r": ("sbuf", [128, 256], "float32"),
-    "m1": ("sbuf", [128, 128], "float32"), "m2": ("sbuf", [128, 64], "float32"),
-    "e1": ("sbuf", [128, 32], "float32"), "e2": ("sbuf", [128, 32], "float32"), "e3": ("sbuf", [128, 32], "float32"),
-    "e12": ("sbuf", [128, 32], "float32"), "e": ("sbuf", [128, 32], "float32"),
-    "cs": ("sbuf", [128, 32], "float32"), "t1": ("sbuf", [128, 32], "float32"), "t2": ("sbuf", [128, 32], "float32"), "t3": ("sbuf", [128, 32], "float32"),
-    "v1": ("sbuf", [128, 32], "float32"), "v2": ("sbuf", [128, 32], "float32"), "v3": ("sbuf", [128, 32], "float32"),
-    "ow": ("sbuf", [128, 32], "uint16"), "l": ("sbuf", [128, 512], "float32"),
-    "lm": ("sbuf", [128, 96], "float32"), "ls": ("sbuf", [128, 96], "float32"), "og": ("sbuf", [128, 24], "uint16"),
-    "b1": ("sbuf", [128, 128], "float32"), "b2": ("sbuf", [128, 64], "float32"), "b3": ("sbuf", [128, 32], "float32"),
-    "d1": ("sbuf", [128, 64], "float32"), "d2": ("sbuf", [128, 64], "float32"), "d3": ("sbuf", [128, 64], "float32"), "w2": ("sbuf", [128, 64], "float32"),
-    "f1": ("sbuf", [128, 32], "float32"), "f2": ("sbuf", [128, 32], "float32"), "f3": ("sbuf", [128, 32], "float32"), "win": ("sbuf", [128, 32], "float32"),
-    "ee": ("sbuf", [128, 256], "float32"), "ep": ("sbuf", [128, 256], "float32"), "ca1": ("sbuf", [128, 256], "float32"),
-    "tt": ("sbuf", [128, 32], "float32"), "tu": ("sbuf", [128, 32], "float32"), "tv": ("sbuf", [128, 32], "float32"), "tw": ("sbuf", [128, 32], "float32"),
-    "st1": ("sbuf", [128, 8], "float32"), "st2": ("sbuf", [128, 8], "float32"),
-    "u": ("sbuf", [128, 256], "float32"), "uv": ("sbuf", [128, 256], "float32"),
-    "x1": ("sbuf", [128, 128], "float32"), "x2": ("sbuf", [128, 64], "float32"), "ix": ("sbuf", [128, 32], "float32"), "it": ("sbuf", [128, 32], "float32"),
-    "bx": ("sbuf", [128, 256], "float32"), "off": ("sbuf", [128, 256], "uint16"),
-    "ps": ("psum", [128, 4096], "float32"),
-    "p": ("sbuf", [128, 6400], "float32"), "ya": ("sbuf", [128, 512], "float32"),
-}
-SEMAPHORES = ["lu", "lx0", "lx1", "lx2", "lx3", "lw", "gi", "v", "s", "pe", "it1", "it2", "st",
-              "asc", "aa", "ab", "ac", "loc"]
+F4, F, B = "float8_e4m3fn_x4", "float32", "bfloat16"
+SCRATCH = {}
+for _names, _w, _t in (
+        ("uw", 64, B), ("xs", 2048, B), ("zt", 560, B), ("wz", 4096, B), ("h", 512, B),
+        ("cz", 140, F4), ("pz", 140, "uint8"), ("cx", 512, F4), ("px", 512, "uint8"), ("cw", 1024, F4), ("pw", 1024, "uint8"),
+        ("ca", 224, F4), ("pa", 224, "uint8"), ("cb", 576, F4), ("pb", 576, "uint8"),
+        ("ia ib", 4, "int32"), ("fa", 4, F), ("g8 kc st1 st2", 8, F), ("v32 ms sm m1 b1 g2 x1 y1", 128, F),
+        ("oz", 36, "uint16"), ("ic c1 i16 r16 one", 32, F), ("ij cj ya", 512, F), ("k4 m4 r4 lm ls", 96, F),
+        ("i256 wt r ep u uv wv bx", 256, F), ("r256 ee cs8", 256, B), ("s2 m2 e3b b2 x2 y2", 64, F), ("l", 528, F),
+        ("e1 e2 e3 e12 e cs t1 t2 t3 v1 v3 tt tu tv tw ix it win", 32, F),
+        ("ow", 32, "uint16"), ("og", 24, "uint16"), ("off", 256, "uint16"), ("p", 6144, F)):
+    for _k in _names.split():
+        SCRATCH[_k] = ("sbuf", [128, _w], _t)
+SCRATCH["ps"] = ("psum", [128, 4096], F)
+SEMAPHORES = ["lu", "lx0", "lx1", "lx2", "lx3", "lw", "lw2", "gi", "v", "s", "pe", "it1", "it2", "st",
+              "asc", "aa", "aap", "ab", "abp", "ac", "loc"]
 
 ADD, SUB, MUL, MAX, MIN = AluOpType.add, AluOpType.subtract, AluOpType.mult, AluOpType.max, AluOpType.min
-GE, GT, EQ = AluOpType.is_ge, AluOpType.is_gt, AluOpType.is_equal
+GE, GT, EQ, AND = AluOpType.is_ge, AluOpType.is_gt, AluOpType.is_equal, AluOpType.bitwise_and
 COPY = ActivationFunctionType.Copy
 
 
@@ -68,6 +40,13 @@ def rank_program(g, core, T, topo):
         call.then_inc(S[q], 1)
         return n[q]
 
+    vw = lambda k: V.wait_ge(S.v, k)
+    vec = lambda call: inc("v", call)
+    tt = lambda out, a, b, op: vec(V.tensor_tensor(out, a, b, op))
+    ts = lambda out, a, s1, op, s2=None, op2=None: vec(V.tensor_scalar(out, a, s1, s2, op, op2) if op2 else V.tensor_scalar(out, a, s1, None, op))
+    scan = lambda out, a, b, o0=MUL, o1=ADD: vec(V.tensor_tensor_scan(out, a, b, 0.0, o0, o1))
+    iota = lambda out, pat, base, cm: inc("gi", g.iota(out, pat, base, cm, allow_small_or_imprecise_dtypes=True))
+
     cores = list(T.cores)
     chips = []
     for c in cores:
@@ -79,283 +58,230 @@ def rank_program(g, core, T, topo):
     mate = [c for c in on(mychip) if c != core][0]
     far = [c for c in cores if topo.chip(c) != mychip]
     same = [on(ch)[kind] for ch in chips if ch != mychip]
-    slot = lambda frm, to: [ch for ch in chips if ch != topo.chip(to)].index(topo.chip(frm))
-    eng_far = [e for e in topo.engines(core, far[0])]
-    for c in far:
-        eng_far = [e for e in eng_far if e in topo.engines(core, c)]
+    slot = lambda frm, to: 192 * [ch for ch in chips if ch != topo.chip(to)].index(topo.chip(frm))
+    eng_far = [e for e in topo.engines(core, mate) if all(e in topo.engines(core, c) for c in far)]
     eng_near = [e for e in topo.engines(core, mate) if e not in eng_far][:4]
-    m_far = sum(1 << e for e in eng_far)
-    m_near = sum(1 << e for e in eng_near)
+    n_far, n_near = len(eng_far), len(eng_near)
     did = lambda c: DstId(rid=topo.addr(c)[0], pnc=topo.addr(c)[1])
 
     def start_of(s):
         c = cores[s]
-        if c == core:
-            return 0
-        if c == mate:
-            return 128
-        return (224 if on(topo.chip(c)).index(c) == kind else 512) + 96 * slot(c, core)
+        if c in (core, mate):
+            return 0 if c == core else 96
+        return 192 + slot(c, core) + (0 if c in same else 96)
 
-    def send(transfers):
-        for t in transfers:
-            n["loc"] += t[0]
-        g.remote_dma_fused([t[1] for t in transfers], local_sem=S.loc)
+    def send(*transfers):
+        n["loc"] += sum(len(m) for m, _, _, _ in transfers)
+        g.remote_dma_fused([RemoteDMATransfer(dst_ids=[did(c) for c, _ in to], dma_engine_mask=sum(1 << e for e in m), remote_sem=sem,
+                                              srcs=[src], dsts=[d for _, d in to], alu_op=0) for m, sem, src, to in transfers], local_sem=S.loc)
 
     Y.dma_start(T.uw[:, 0:64], T.us[:, 0:64]).then_inc(S.lu, 16)
-    for k in (0, 2):
-        Y.dma_start(T.xs[:, 512 * k:512 * k + 512], T.x[:, 512 * k:512 * k + 512]).then_inc(S["lx%d" % k], 16)
-    for k in (1, 3):
-        A.dma_start(T.xs[:, 512 * k:512 * k + 512], T.x[:, 512 * k:512 * k + 512]).then_inc(S["lx%d" % k], 16)
+    for q, k in ((A, 0), (Y, 1), (A, 2), (Y, 3)):
+        q.dma_start(T.xs[:, 512 * k:512 * k + 512], T.x[:, 512 * k:512 * k + 512]).then_inc(S["lx%d" % k], 16)
 
-    iota = lambda out, pat, base, cm: inc("gi", g.iota(out, pat, base, cm, allow_small_or_imprecise_dtypes=True))
-    g.iota(T.ia[:, 0:1], [[0, 1]], 0, 1).then_inc(S.gi, 1)
-    g.iota(T.ia[:, 1:2], [[0, 1]], 0, 32).then_inc(S.gi, 1)
-    n["gi"] = 2
-    iota(T.g8[:, :], [[4, 8]], 0, 0)
-    k_i0 = n["gi"]
-    iota(T.v32[:, :], [[1, 4], [0, 32]], 0, 0)
-    k_v32 = n["gi"]
-    iota(T.ic[:, :], [[1, 32]], -512, 0)
+    inc("gi", g.iota(T.ia[:, 0:1], [[0, 1]], 0, 1))
+    inc("gi", g.iota(T.ia[:, 1:2], [[0, 1]], 0, 32))
+    k_a = iota(T.g8[:, :], [[4, 8]], 0, 0)
+    k_b = iota(T.v32[:, :], [[1, 4], [0, 32]], 0, 0)
+    iota(T.ic[:, :], [[-1, 32]], 512, 0)
     iota(T.k4[:, :], [[0, 24], [1, 4]], 0, 0)
     iota(T.i16[:, :], [[0, 2], [1, 16]], 0, 0)
     iota(T.ij[:, :], [[4, 32], [128, 16]], 0, 0)
-    iota(T.i256[:, :], [[0, 8], [1, 32]], 0, 0)
-    k_iall = n["gi"]
+    k_c = iota(T.i256[:, :], [[0, 8], [1, 32]], 0, 0)
 
-    k = inc("v", V.memset(T.oz[:, :], 32))
-    V.wait_ge(S.gi, k_i0)
-    AND = AluOpType.bitwise_and
-    inc("v", V.tensor_scalar(T.ib[:, 0:1], T.ia[:, 0:1], 3, None, AND))
-    inc("v", V.tensor_scalar(T.ib[:, 1:2], T.ia[:, 1:2], 511, None, AND))
-    inc("v", V.tensor_scalar(T.ib[:, 2:3], T.ia[:, 0:1], 12, 2, AND, AluOpType.arith_shift_right))
-    V.wait_ge(S.v, n["v"])
-    inc("v", V.tensor_copy(T.fa[:, 0:3], T.ib[:, 0:3]))
-    V.wait_ge(S.v, n["v"])
-    v_oz = inc("v", V.tensor_scalar(T.oz[:, 3:32:4], T.g8[:, :], T.fa[:, 0:1], None, ADD))
-    v_wz = inc("v", V.memset(T.wz[:, :], 0.0))
-    V.wait_ge(S.gi, k_v32)
-    inc("v", V.tensor_scalar(T.ms[:, :], T.v32[:, :], T.fa[:, 0:1], None, EQ))
-    inc("v", V.memset(T.h[:, 384:512], 0.0))
+    vec(V.memset(T.oz[:, :], 32))
+    V.wait_ge(S.gi, k_a)
+    ts(T.ib[:, 0:1], T.ia[:, 0:1], 3, AND)
+    ts(T.ib[:, 1:2], T.ia[:, 1:2], 511, AND)
+    vw(ts(T.ib[:, 2:3], T.ia[:, 0:1], 12, AND, 2, AluOpType.arith_shift_right))
+    vw(vec(V.tensor_copy(T.fa[:, 0:3], T.ib[:, 0:3])))
+    v_oz = ts(T.oz[:, 3:32:4], T.g8[:, :], T.fa[:, 0:1], ADD)
+    v_wz = vec(V.memset(T.wz[:, 0:2048], 0.0))
+    V.wait_ge(S.gi, k_b)
+    ts(T.ms[:, :], T.v32[:, :], T.fa[:, 0:1], EQ)
+    vec(V.memset(T.h[:, 0:128], 0.0))
 
     A.wait_ge(S.lu, 16)
     A.wait_ge(S.v, v_oz)
-    s_zt = inc("s", A.activation(T.zt[:, 0:560], T.uw[:, 0:64].indirect(T.oz[:, 0:35]), COPY))
+    s_zt = inc("s", A.activation(T.zt[:, 288:560], T.uw[:, 0:64].indirect(T.oz[:, 18:35]), COPY))
+    V.wait_ge(S.lu, 16)
+    vw(v_oz)
+    k = vec(V.tensor_copy(T.zt[:, 0:288], T.uw[:, 0:64].indirect(T.oz[:, 0:18])))
+    vw(k)
+    V.wait_ge(S.s, s_zt)
+    vec(V.quantize_mx(T.cz[:, :], T.pz[:, :], T.zt[:, :]))
+
+    def load_w(heads, sem):
+        for q in heads:
+            Y.dma_start(T.wz[16 * q:16 * q + 16, 512 * q:512 * q + 512], T.w[16 * q:16 * q + 16, :]).then_inc(sem, 16)
 
     Y.wait_ge(S.v, v_wz)
-    for q in range(8):
-        Y.dma_start(T.wz[16 * q:16 * q + 16, 512 * q:512 * q + 512], T.w[16 * q:16 * q + 16, :]).then_inc(S.lw, 16)
+    load_w(range(4), S.lw)
 
-    V.wait_ge(S.s, s_zt)
-    inc("v", V.quantize_mx(T.cz[:, :], T.pz[:, :], T.zt[:, :]))
     for q in range(4):
         V.wait_ge(S["lx%d" % q], 16)
-        kq = inc("v", V.quantize_mx(T.cx[:, 128 * q:128 * q + 128], T.px[:, 128 * q:128 * q + 128], T.xs[:, 512 * q:512 * q + 512]))
-        P.wait_ge(S.v, kq)
-        a = 12 - 4 * q
+        a, b = 12 - 4 * q, 128 * q
+        P.wait_ge(S.v, vec(V.quantize_mx(T.cx[:, b:b + 128], T.px[:, b:b + 128], T.xs[:, 4 * b:4 * b + 512])))
         k_sc = inc("pe", P.matmul_mx(T.ps[:, 3584:3712], T.cz[:, a:a + 128], T.pz[:, a:a + 128],
-                                     T.cx[:, 128 * q:128 * q + 128], T.px[:, 128 * q:128 * q + 128], q == 0, q == 3))
+                                     T.cx[:, b:b + 128], T.px[:, b:b + 128], q == 0, q == 3))
     V.wait_ge(S.pe, k_sc)
     me = bitrev(rank)
-    own = T.r[:, 32 * me:32 * me + 32]
-    V.wait_ge(S.v, inc("v", V.tensor_tensor(T.sm[:, :], T.ps[:, 3584:3712], T.ms[:, :], MUL)))
-    V.wait_ge(S.v, inc("v", V.tensor_tensor(T.s2[:, :], T.sm[:, 0:64], T.sm[:, 64:128], ADD)))
-    v_own = inc("v", V.tensor_tensor(own, T.s2[:, 0:32], T.s2[:, 32:64], ADD))
-    g.wait_ge(S.v, v_own)
-    send([(len(eng_far), RemoteDMATransfer(dst_ids=[did(c) for c in far], dma_engine_mask=m_far, remote_sem=S.asc,
-                                           srcs=[own], dsts=[own] * len(far), alu_op=0)),
-          (len(eng_near), RemoteDMATransfer(dst_ids=[did(mate)], dma_engine_mask=m_near, remote_sem=S.asc,
-                                            srcs=[own], dsts=[own], alu_op=0))])
-
-    V.wait_ge(S.gi, k_iall)
-    inc("v", V.tensor_scalar(T.c1[:, :], T.ic[:, :], T.fa[:, 0:1] if False else T.fa[:, 1:2], None, ADD))
-    kc1 = n["v"]
-    inc("v", V.tensor_scalar(T.cj[:, :], T.ij[:, :], T.fa[:, 0:1], None, ADD))
-    inc("v", V.tensor_scalar(T.m4[:, :], T.k4[:, :], T.fa[:, 2:3], None, EQ))
-    inc("v", V.tensor_scalar(T.r4[:, :], T.k4[:, :], 1.0, None, MIN))
-    inc("v", V.tensor_scalar(T.r16[:, :], T.i16[:, :], 1.0, None, MIN))
-    inc("v", V.tensor_scalar(T.r256[:, :], T.i256[:, :], 1.0, None, MIN))
-    inc("v", V.memset(T.one[:, :], 1.0))
-    inc("v", V.memset(T.tt[:, :], 0.0))
-    for s in range(8):
-        inc("v", V.memset(T.kc[:, s:s + 1], float(start_of(s) - 1)))
-    V.wait_ge(S.v, kc1)
-    inc("v", V.tensor_scalar(T.c2[:, :], T.c1[:, :], -1.0, -1.0, MUL, ADD))
-    V.wait_ge(S.lw, 128)
-    inc("v", V.quantize_mx(T.cw[:, 0:512], T.pw[:, 0:512], T.wz[:, 0:2048]))
-    v_w = inc("v", V.quantize_mx(T.cw[:, 512:1024], T.pw[:, 512:1024], T.wz[:, 2048:4096]))
-
-    vw = lambda k: V.wait_ge(S.v, k)
     R = lambda b, q=1: T.r[:, 32 * b:32 * (b + q)]
-    V.wait_ge(S.asc, len(eng_far) * len(far) + len(eng_near))
-    vw(n["v"])
-    sib = lambda bit: GE if not bit else GT
-    lo, hi = me & 3, me & 1
-    k1 = inc("v", V.tensor_tensor(T.m1[:, :], R(0, 4), R(4, 4), MAX))
-    inc("v", V.tensor_tensor(T.e1[:, :], own, R(me ^ 4), sib(me & 4)))
-    vw(k1)
-    k2 = inc("v", V.tensor_tensor(T.m2[:, :], T.m1[:, 0:64], T.m1[:, 64:128], MAX))
-    ke2 = inc("v", V.tensor_tensor(T.e2[:, :], T.m1[:, 32 * lo:32 * lo + 32], T.m1[:, 32 * (lo ^ 2):32 * (lo ^ 2) + 32], sib(me & 2)))
-    vw(k2)
-    k3 = inc("v", V.tensor_tensor(T.e3[:, :], T.m2[:, 32 * hi:32 * hi + 32], T.m2[:, 32 * (hi ^ 1):32 * (hi ^ 1) + 32], sib(me & 1)))
-    vw(ke2)
-    k4 = inc("v", V.tensor_tensor(T.e12[:, :], T.e1[:, :], T.e2[:, :], MUL))
-    vw(k4)
-    ke = inc("v", V.tensor_tensor(T.e[:, :], T.e12[:, :], T.e3[:, :], MUL))
-    vw(ke)
-    kcs = inc("v", V.tensor_tensor_scan(T.cs[:, :], T.one[:, :], T.e[:, :], 0.0, MUL, ADD))
-    kv1 = inc("v", V.tensor_tensor(T.v1[:, :], T.e[:, :], T.c1[:, :], MUL))
-    vw(kcs)
-    kt1 = inc("v", V.transpose(T.t1[:, :], T.cs[:, :]))
-    vw(kv1)
-    kv2 = inc("v", V.tensor_tensor(T.v2[:, :], T.v1[:, :], T.c2[:, :], ADD))
-    vw(kt1)
-    kt2 = inc("v", V.tensor_tensor_scan(T.t2[:, :], T.r16[:, :], T.t1[:, :], 0.0, MUL, ADD))
-    vw(kv2)
-    kv3 = inc("v", V.tensor_tensor(T.v3[:, :], T.v2[:, :], T.cs[:, :], ADD))
-    vw(kt2)
-    kt3 = inc("v", V.transpose(T.t3[:, :], T.t2[:, :]))
-    vw(kt3)
-    k = inc("v", V.tensor_scalar(T.ow[:, :], T.v3[:, :], T.t3[:, 31:32], T.cs[:, 31:32], ADD, SUB))
-    vw(k)
-    k = inc("v", V.tensor_copy(T.l[:, 0:512].indirect(T.ow[:, 0:32]), T.cj[:, :]))
-    vw(k)
-    k = inc("v", V.tensor_tensor(T.lm[:, :], T.l[:, 0:96], T.m4[:, :], MUL))
-    vw(k)
-    k = inc("v", V.tensor_tensor_scan(T.ls[:, :], T.r4[:, :], T.lm[:, :], 0.0, MUL, ADD))
-    vw(k)
-    v_og = inc("v", V.tensor_copy(T.og[:, :], T.ls[:, 3:96:4]))
-    vw(v_og)
-    k = inc("v", V.tensor_copy(T.h[:, 0:192], T.xs[:, 0:2048].indirect(T.og[:, 0:12])))
-    A.wait_ge(S.v, v_og)
-    s_h = inc("s", A.activation(T.h[:, 192:384], T.xs[:, 0:2048].indirect(T.og[:, 12:24]), COPY))
-    vw(k)
-    V.wait_ge(S.s, s_h)
-    v_q = inc("v", V.quantize_mx(T.ca[:, 0:128], T.pa[:, 0:128], T.h[:, :]))
-    g.wait_ge(S.v, v_q)
-    oc, op = T.ca[:, 0:96].bitcast(dt.uint8), T.pa[:, 0:96]
-    for src, to_far, to_near in (
-            (oc, [T.cb[:, 96 * slot(core, c):96 * slot(core, c) + 96].bitcast(dt.uint8) for c in same], T.ca[:, 128:224].bitcast(dt.uint8)),
-            (op, [T.pb[:, 96 * slot(core, c):96 * slot(core, c) + 96] for c in same], T.pa[:, 128:224])):
-        send([(len(eng_far), RemoteDMATransfer(dst_ids=[did(c) for c in same], dma_engine_mask=m_far, remote_sem=S.ab,
-                                               srcs=[src], dsts=to_far, alu_op=0)),
-              (len(eng_near), RemoteDMATransfer(dst_ids=[did(mate)], dma_engine_mask=m_near, remote_sem=S.aa,
-                                                srcs=[src], dsts=[to_near], alu_op=0))])
-    n_aa, n_ab, n_ac = 2 * len(eng_near), 2 * len(eng_far) * len(same), len(eng_far) + len(eng_near)
-    g.wait_ge(S.ab, n_ab)
-    send([(len(eng_far), RemoteDMATransfer(dst_ids=[did(mate)], dma_engine_mask=m_far, remote_sem=S.ac,
-                                           srcs=[T.cb[:, :].bitcast(dt.uint8)], dsts=[T.cc[:, :].bitcast(dt.uint8)], alu_op=0))])
-    send([(len(eng_near), RemoteDMATransfer(dst_ids=[did(mate)], dma_engine_mask=m_near, remote_sem=S.ac,
-                                            srcs=[T.pb[:, :]], dsts=[T.pc[:, :]], alu_op=0))])
+    own = R(me)
+    vw(tt(T.sm[:, :], T.ps[:, 3584:3712], T.ms[:, :], MUL))
+    vw(tt(T.s2[:, :], T.sm[:, 0:64], T.sm[:, 64:128], ADD))
+    g.wait_ge(S.v, tt(own, T.s2[:, 0:32], T.s2[:, 32:64], ADD))
+    near2 = eng_near[:2]
+    send((eng_far, S.asc, own, [(c, own) for c in far]), (near2, S.asc, own, [(mate, own)]))
 
-    kb1 = inc("v", V.tensor_tensor(T.b1[:, :], R(4, 4), R(0, 4), GT))
-    inc("v", V.tensor_tensor(T.b2[:, :], T.m1[:, 64:128], T.m1[:, 0:64], GT))
-    inc("v", V.tensor_tensor(T.b3[:, :], T.m2[:, 32:64], T.m2[:, 0:32], GT))
-    vw(kb1)
-    k = inc("v", V.tensor_tensor(T.d1[:, :], T.b1[:, 64:128], T.b1[:, 0:64], SUB))
+    v_wz = vec(V.memset(T.wz[:, 2048:4096], 0.0))
+    Y.wait_ge(S.v, v_wz)
+    load_w(range(4, 8), S.lw2)
+    V.wait_ge(S.gi, k_c)
+    ts(T.c1[:, :], T.ic[:, :], T.fa[:, 1:2], SUB)
+    ts(T.cj[:, :], T.ij[:, :], T.fa[:, 0:1], ADD)
+    ts(T.m4[:, :], T.k4[:, :], T.fa[:, 2:3], EQ)
+    ts(T.r4[:, :], T.k4[:, :], 1.0, MIN)
+    ts(T.r16[:, :], T.i16[:, :], 1.0, MIN)
+    ts(T.r256[:, :], T.i256[:, :], 1.0, MIN)
+    vec(V.memset(T.one[:, :], 1.0))
+    vec(V.memset(T.tt[:, :], 0.0))
+    V.wait_ge(S.lw, 64)
+    vec(V.quantize_mx(T.cw[:, 0:512], T.pw[:, 0:512], T.wz[:, 0:2048]))
+    for b in range(8):
+        vec(V.memset(T.kc[:, b:b + 1], float(start_of(bitrev(b)) + 96)))
+        vec(V.memset(T.wt[:, 32 * b:32 * b + 32], float(bitrev(b))))
+    V.wait_ge(S.lw2, 64)
+    vec(V.quantize_mx(T.cw[:, 512:1024], T.pw[:, 512:1024], T.wz[:, 2048:4096]))
+
+    V.wait_ge(S.asc, n_far * len(far) + len(near2))
+    vw(n["v"])
+    half = lambda t, k: t[:, 32 * k:32 * k + 32]
+    lo, hi = me & 3, me & 1
+    vw(tt(T.m1[:, :], R(0, 4), R(4, 4), MAX))
+    tt(T.e1[:, :], own, R(me ^ 4), GT if me & 4 else GE)
+    k = tt(T.m2[:, :], T.m1[:, 0:64], T.m1[:, 64:128], MAX)
+    k2 = tt(T.e2[:, :], half(T.m1, lo), half(T.m1, lo ^ 2), GT if me & 2 else GE)
     vw(k)
-    k = inc("v", V.tensor_scalar(T.d2[:, :], T.d1[:, :], 2.0, None, ADD))
+    k = tt(T.e3[:, :], half(T.m2, hi), half(T.m2, hi ^ 1), GT if me & 1 else GE)
+    vw(k2)
+    vw(tt(T.e12[:, :], T.e1[:, :], T.e2[:, :], MUL))
+    vw(tt(T.e[:, :], T.e12[:, :], T.e3[:, :], MUL))
+    k = scan(T.cs[:, :], T.one[:, :], T.e[:, :], ADD, SUB)
+    k2 = tt(T.v1[:, :], T.e[:, :], T.c1[:, :], MUL)
     vw(k)
-    k = inc("v", V.tensor_tensor(T.d3[:, :], T.d2[:, :], T.b2[:, :], MUL))
+    k = vec(V.transpose(T.t1[:, :], T.cs[:, :]))
+    vw(k2)
+    k2 = tt(T.v3[:, :], T.v1[:, :], T.cs[:, :], ADD)
     vw(k)
-    k = inc("v", V.tensor_tensor(T.w2[:, :], T.d3[:, :], T.b1[:, 0:64], ADD))
-    vw(k)
-    k = inc("v", V.tensor_tensor(T.f1[:, :], T.w2[:, 32:64], T.w2[:, 0:32], SUB))
-    vw(k)
-    k = inc("v", V.tensor_scalar(T.f2[:, :], T.f1[:, :], 4.0, None, ADD))
-    vw(k)
-    k = inc("v", V.tensor_tensor(T.f3[:, :], T.f2[:, :], T.b3[:, :], MUL))
-    vw(k)
-    v_win = inc("v", V.tensor_tensor(T.win[:, :], T.f3[:, :], T.w2[:, 0:32], ADD))
-    vw(v_win)
-    for s in range(8):
-        v_ee = inc("v", V.tensor_scalar(T.ee[:, 32 * s:32 * s + 32], T.win[:, :], float(s), None, EQ))
+    vw(scan(T.t2[:, :], T.r16[:, :], T.t1[:, :]))
+    vw(vec(V.transpose(T.t3[:, :], T.t2[:, :])))
+    vw(ts(T.ow[:, :], T.v3[:, :], T.t3[:, 31:32], ADD, T.cs[:, 31:32], SUB))
+    vw(vec(V.tensor_copy(T.l[:, 0:528].indirect(T.ow[:, 0:32]), T.cj[:, :])))
+    vw(tt(T.lm[:, :], T.l[:, 417:513], T.m4[:, :], MUL))
+    vw(scan(T.ls[:, :], T.r4[:, :], T.lm[:, :]))
+    v_og = vec(V.tensor_copy(T.og[:, :], T.ls[:, 3:96:4]))
+    A.wait_ge(S.v, v_og)
+    s_h = inc("s", A.activation(T.h[:, 320:512], T.xs[:, 0:2048].indirect(T.og[:, 12:24]), COPY))
+    vw(v_og)
+    vw(vec(V.tensor_copy(T.h[:, 128:320], T.xs[:, 0:2048].indirect(T.og[:, 0:12]))))
+    V.wait_ge(S.s, s_h)
+    v_q = vec(V.quantize_mx(T.ca[:, 0:128], T.pa[:, 0:128], T.h[:, :]))
+    g.wait_ge(S.v, v_q)
+    by = lambda t, a: t[:, a:a + 96].bitcast(dt.uint8)
+    send((eng_far, S.ab, by(T.ca, 32), [(c, by(T.cb, slot(core, c))) for c in same]))
+    send((eng_near, S.aap, T.pa[:, 32:128], [(mate, T.pa[:, 128:224])]))
+    send((eng_near, S.aa, by(T.ca, 32), [(mate, by(T.ca, 128))]))
+    g.wait_ge(S.aap, n_near)
+    send((eng_far, S.abp, T.pa[:, 32:224], [(c, T.pb[:, slot(core, c):slot(core, c) + 192]) for c in same]))
+    g.wait_ge(S.ab, n_far * len(same))
+    on_with = [eng_far[:n_far // 2], eng_far[n_far // 2:], eng_near]
+    send(*[(on_with[k], S.ac, by(T.cb, 192 * k), [(mate, by(T.cb, 192 * k + 96))]) for k in range(len(same))])
+
+    tt(half(T.e3b, 0), half(T.m2, 0), half(T.m2, 1), GE)
+    tt(half(T.e3b, 1), half(T.m2, 1), half(T.m2, 0), GT)
+    k2 = tt(T.b2[:, :], T.m1[:, 64:128], T.m1[:, 0:64], GT)
+    tt(T.b1[:, :], R(4, 4), R(0, 4), GT)
+    vw(k2)
+    vw(tt(T.g2[:, 64:128], T.e3b[:, :], T.b2[:, :], MUL))
+    vw(tt(T.g2[:, 0:64], T.e3b[:, :], T.g2[:, 64:128], SUB))
+    vw(tt(T.ee[:, 128:256], T.g2[:, :], T.b1[:, :], MUL))
+    v_ee = tt(T.ee[:, 0:128], T.g2[:, :], T.ee[:, 128:256], SUB)
     A.wait_ge(S.v, v_ee)
     s_ep = inc("s", A.activation(T.ep[:, :], T.ee[:, :], COPY))
     vw(v_ee)
-    k = inc("v", V.tensor_tensor_scan(T.ca1[:, :], T.r256[:, :], T.ee[:, :], 0.0, MUL, ADD))
+    vw(scan(T.cs8[:, :], T.r256[:, :], T.ee[:, :], MUL, SUB))
+    vw(vec(V.tensor_copy(T.tt[:, 0:8], T.cs8[:, 31:256:32])))
+    k = vec(V.transpose(T.tu[:, :], T.tt[:, :]))
+    tt(T.st1[:, :], T.kc[:, :], T.tt[:, 0:8], SUB)
     vw(k)
-    k = inc("v", V.tensor_copy(T.tt[:, 0:8], T.ca1[:, 31:256:32]))
-    vw(k)
-    k = inc("v", V.transpose(T.tu[:, :], T.tt[:, :]))
-    vw(k)
-    k = inc("v", V.tensor_tensor_scan(T.tv[:, :], T.r16[:, :], T.tu[:, :], 0.0, MUL, ADD))
-    inc("v", V.tensor_tensor(T.st1[:, :], T.kc[:, :], T.tt[:, 0:8], SUB))
-    vw(k)
-    k = inc("v", V.transpose(T.tw[:, :], T.tv[:, :]))
-    vw(k)
-    k = inc("v", V.tensor_tensor(T.st2[:, :], T.st1[:, :], T.tw[:, 0:8], ADD))
-    vw(k)
+    vw(scan(T.tv[:, :], T.r16[:, :], T.tu[:, :]))
+    vw(vec(V.transpose(T.tw[:, :], T.tv[:, :])))
+    vw(tt(T.st2[:, :], T.st1[:, :], T.tw[:, 0:8], ADD))
     V.wait_ge(S.s, s_ep)
-    k = inc("v", V.tensor_tensor(T.ep[:, 0:256:32], T.ep[:, 0:256:32], T.st2[:, :], ADD))
-    vw(k)
-    k = inc("v", V.tensor_tensor_scan(T.u[:, :], T.r256[:, :], T.ep[:, :], 0.0, MUL, ADD))
-    vw(k)
-    k = inc("v", V.tensor_tensor(T.uv[:, :], T.u[:, :], T.ee[:, :], MUL))
-    vw(k)
-    k = inc("v", V.tensor_tensor(T.x1[:, :], T.uv[:, 0:128], T.uv[:, 128:256], ADD))
-    vw(k)
-    k = inc("v", V.tensor_tensor(T.x2[:, :], T.x1[:, 0:64], T.x1[:, 64:128], ADD))
-    vw(k)
-    k = inc("v", V.tensor_tensor(T.ix[:, :], T.x2[:, 0:32], T.x2[:, 32:64], ADD))
-    vw(k)
-    v_it = inc("v", V.transpose(T.it[:, :], T.ix[:, :]))
-    Y.wait_ge(S.v, v_it)
-    for q in range(4):
-        for b in range(2):
-            Y.dma_start(T.bx[0:16, 128 * b + 32 * q:128 * b + 32 * q + 32], T.it[32 * q + 16 * b:32 * q + 16 * b + 16, :]).then_inc(S.it1, 16)
+    vw(tt(T.ep[:, 0:256:32], T.ep[:, 0:256:32], T.st2[:, :], SUB))
+    vw(scan(T.u[:, :], T.r256[:, :], T.ep[:, :], MUL, SUB))
+    vw(tt(T.uv[:, :], T.u[:, :], T.ee[:, :], MUL))
+    vw(tt(T.x1[:, :], T.uv[:, 0:128], T.uv[:, 128:256], ADD))
+    vw(tt(T.x2[:, :], T.x1[:, 0:64], T.x1[:, 64:128], ADD))
+    vw(tt(T.ix[:, :], T.x2[:, 0:32], T.x2[:, 32:64], ADD))
+    v_it = vec(V.transpose(T.it[:, :], T.ix[:, :]))
+    for q, b in ((Y, 0), (A, 1)):
+        q.wait_ge(S.v, v_it)
+        for k in range(4):
+            q.dma_start(T.bx[0:16, 128 * b + 32 * k:128 * b + 32 * k + 32], T.it[32 * k + 16 * b:32 * k + 16 * b + 16, :]).then_inc(S.it1, 16)
     Y.wait_ge(S.it1, 128)
     for q in range(1, 8):
         Y.dma_start(T.bx[16 * q:16 * q + 16, :], T.bx[0:16, :]).then_inc(S.it2, 16)
+    vw(tt(T.wv[:, :], T.ee[:, :], T.wt[:, :], MUL))
+    vw(tt(T.y1[:, :], T.wv[:, 0:128], T.wv[:, 128:256], ADD))
+    vw(tt(T.y2[:, :], T.y1[:, 0:64], T.y1[:, 64:128], ADD))
+    Y.wait_ge(S.v, tt(T.win[:, :], T.y2[:, 0:32], T.y2[:, 32:64], ADD))
     Y.dma_start(T.wn[:, :], T.win[:, :]).then_inc(S.st, 16)
 
-    bank = lambda q, w: T.ps[:, 512 * q:512 * q + w]
-    wq = lambda q: (T.cw[:, 128 * q:128 * q + 128], T.pw[:, 128 * q:128 * q + 128])
-    done = [None] * 8
+    freed = [None] * 8
 
-    def product(q, codes, plane, w):
-        if done[q]:
-            P.wait_ge(S[done[q][0]], done[q][1])
-        return inc("pe", P.matmul_mx(bank(q, w), wq(q)[0], wq(q)[1], codes[:, 0:w], plane[:, 0:w], True, True))
-
-    def out_of(q, at, w, k, vec):
-        eng, key = (V, "v") if vec else (A, "s")
-        eng.wait_ge(S.pe, k)
-        dst = T.p[:, 800 * q + at:800 * q + at + w]
-        done[q] = (key, inc(key, V.tensor_copy(dst, bank(q, w)) if vec else A.activation(dst, bank(q, w), COPY)))
+    def product(q, bank, codes, plane, a, w, at):
+        if freed[bank]:
+            P.wait_ge(S.s, freed[bank])
+        src, out = T.ps[:, 512 * bank:512 * bank + w], T.p[:, 768 * q + at:768 * q + at + w]
+        k = inc("pe", P.matmul_mx(src, T.cw[:, 128 * q:128 * q + 128], T.pw[:, 128 * q:128 * q + 128],
+                                  codes[:, a:a + w], plane[:, a:a + w], True, True))
+        A.wait_ge(S.pe, k)
+        freed[bank] = inc("s", A.activation(out, src, COPY))
+        return freed[bank]
 
     P.wait_ge(S.v, v_q)
-    P.wait_ge(S.aa, n_aa)
+    P.wait_ge(S.aap, n_near)
+    P.wait_ge(S.aa, n_near)
     for q in range(8):
-        out_of(q, 0, 224, product(q, T.ca, T.pa, 224), False)
-    P.wait_ge(S.ab, n_ab)
-    for q in (0, 4, 1, 5, 2, 6, 3, 7):
-        out_of(q, 224, 288, product(q, T.cb, T.pb, 288), q > 3)
-    v_b = n["v"]
-    P.wait_ge(S.ac, n_ac)
-    for q in range(8):
-        out_of(q, 512, 288, product(q, T.cc, T.pc, 288), False)
-
-    V.wait_ge(S.it2, 112)
+        product(q, q, T.ca, T.pa, 32, 192, 0)
     V.wait_ge(S.it1, 128)
-    inc("v", V.tensor_copy(T.off[:, 0:256:2], T.bx[:, 0:128]))
-    inc("v", V.tensor_copy(T.off[:, 1:256:2], T.bx[:, 128:256]))
+    V.wait_ge(S.it2, 112)
+    vec(V.tensor_copy(T.off[:, 0:256:2], T.bx[:, 0:128]))
+    vec(V.tensor_copy(T.off[:, 1:256:2], T.bx[:, 128:256]))
+    P.wait_ge(S.ab, n_far * len(same))
+    P.wait_ge(S.abp, n_far * len(same))
+    P.wait_ge(S.ac, n_far + n_near)
+    ready = []
+    for q in range(8):
+        ready.append([product(q, (2 * q + k) % 8, T.cb, T.pb, 288 * k, 288, 192 + 288 * k) for k in range(2)][1])
+
     vw(n["v"])
 
     def pick(q, a, b, last):
         out = T.ya[:, a:b]
-        src = T.p[:, 800 * q:800 * q + 800].indirect(T.off[:, 32 * q + a // 16:32 * q + b // 16])
+        src = T.p[:, 768 * q:768 * q + 768].indirect(T.off[:, 32 * q + a // 16:32 * q + b // 16])
+        V.wait_ge(S.s, ready[q])
         if last:
             vw(last)
-        return inc("v", V.tensor_tensor(out, src, out, ADD) if last else V.tensor_copy(out, src))
+        return vec(V.tensor_tensor(out, src, out, ADD) if last else V.tensor_copy(out, src))
 
     last = 0
     for q in range(6):
-        V.wait_ge(S.s, done[q][1])
         last = pick(q, 0, 512, last)
     for a in (0, 256):
-        for q in (6, 7):
-            V.wait_ge(S.s, done[q][1])
-            k = pick(q, a, a + 256, last if q == 6 else k)
+        k = pick(7, a, a + 256, pick(6, a, a + 256, last))
         Y.wait_ge(S.v, k)
         Y.dma_start(T.y[:, a:a + 256], T.ya[:, a:a + 256]).then_inc(S.st, 16)
     Y.wait_ge(S.st, 48)

@@ -15,7 +15,7 @@ for _names, _w, _t in (
     for _k in _names.split():
         SCRATCH[_k] = ("sbuf", [128, _w], _t)
 SCRATCH["ps"] = ("psum", [128, 4096], F)
-SEMAPHORES = ["lu", "lx0", "lx1", "lx2", "lx3", "lw", "lw2", "gi", "v", "s", "pe", "it1", "it2", "st",
+SEMAPHORES = ["lu", "lx0", "lx1", "lx2", "lx3", "lw", "gi", "v", "s", "pe", "it1", "it2", "st",
               "asc", "aa", "aap", "ab", "abp", "ac", "loc"]
 
 ADD, SUB, MUL, MAX, MIN = AluOpType.add, AluOpType.subtract, AluOpType.mult, AluOpType.max, AluOpType.min
@@ -90,40 +90,42 @@ def rank_program(g, core, T, topo):
     k_c = iota(T.i256[:, :], [[0, 8], [1, 32]], 0, 0)
 
     vec(V.memset(T.oz[:, :], 32))
+    v_z = vec(V.memset(T.wz[:, 0:1024], 0.0))
+    A.wait_ge(S.v, v_z)
+    s_wz = inc("s", A.activation(T.wz[:, 3072:4096], T.wz[:, 0:1024], COPY))
     V.wait_ge(S.gi, k_a)
     ts(T.ib[:, 0:1], T.ia[:, 0:1], 3, AND)
     ts(T.ib[:, 1:2], T.ia[:, 1:2], 511, AND)
     vw(ts(T.ib[:, 2:3], T.ia[:, 0:1], 12, AND, 2, AluOpType.arith_shift_right))
     vw(vec(V.tensor_copy(T.fa[:, 0:3], T.ib[:, 0:3])))
     v_oz = ts(T.oz[:, 3:32:4], T.g8[:, :], T.fa[:, 0:1], ADD)
-    v_wz = vec(V.memset(T.wz[:, 0:2048], 0.0))
+    vec(V.memset(T.wz[:, 1024:2048], 0.0))
     V.wait_ge(S.gi, k_b)
     ts(T.ms[:, :], T.v32[:, :], T.fa[:, 0:1], EQ)
-    vec(V.memset(T.h[:, 0:128], 0.0))
 
     A.wait_ge(S.lu, 16)
     A.wait_ge(S.v, v_oz)
-    s_zt = inc("s", A.activation(T.zt[:, 288:560], T.uw[:, 0:64].indirect(T.oz[:, 18:35]), COPY))
-    V.wait_ge(S.lu, 16)
-    vw(v_oz)
-    k = vec(V.tensor_copy(T.zt[:, 0:288], T.uw[:, 0:64].indirect(T.oz[:, 0:18])))
-    vw(k)
-    V.wait_ge(S.s, s_zt)
-    vec(V.quantize_mx(T.cz[:, :], T.pz[:, :], T.zt[:, :]))
-
-    def load_w(heads, sem):
-        for q in heads:
-            Y.dma_start(T.wz[16 * q:16 * q + 16, 512 * q:512 * q + 512], T.w[16 * q:16 * q + 16, :]).then_inc(sem, 16)
-
-    Y.wait_ge(S.v, v_wz)
-    load_w(range(4), S.lw)
+    s_zt = inc("s", A.activation(T.zt[:, :], T.uw[:, 0:64].indirect(T.oz[:, 0:35]), COPY))
 
     for q in range(4):
+        if q == 3:
+            V.wait_ge(S.s, s_zt)
+            vec(V.quantize_mx(T.cz[:, :], T.pz[:, :], T.zt[:, :]))
         V.wait_ge(S["lx%d" % q], 16)
+        v_x = vec(V.quantize_mx(T.cx[:, 128 * q:128 * q + 128], T.px[:, 128 * q:128 * q + 128], T.xs[:, 512 * q:512 * q + 512]))
+        if q == 0:
+            v_wz = vec(V.memset(T.wz[:, 2048:3072], 0.0))
+    for q in range(4):
         a, b = 12 - 4 * q, 128 * q
-        P.wait_ge(S.v, vec(V.quantize_mx(T.cx[:, b:b + 128], T.px[:, b:b + 128], T.xs[:, 4 * b:4 * b + 512])))
+        P.wait_ge(S.v, v_x if q == 3 else v_x - 1)
         k_sc = inc("pe", P.matmul_mx(T.ps[:, 3584:3712], T.cz[:, a:a + 128], T.pz[:, a:a + 128],
                                      T.cx[:, b:b + 128], T.px[:, b:b + 128], q == 0, q == 3))
+
+    Y.wait_ge(S.v, v_wz)
+    Y.wait_ge(S.s, s_wz)
+    for q in range(8):
+        Y.dma_start(T.wz[16 * q:16 * q + 16, 512 * q:512 * q + 512], T.w[16 * q:16 * q + 16, :]).then_inc(S.lw, 16)
+
     V.wait_ge(S.pe, k_sc)
     me = bitrev(rank)
     R = lambda b, q=1: T.r[:, 32 * b:32 * (b + q)]
@@ -134,9 +136,7 @@ def rank_program(g, core, T, topo):
     near2 = eng_near[:2]
     send((eng_far, S.asc, own, [(c, own) for c in far]), (near2, S.asc, own, [(mate, own)]))
 
-    v_wz = vec(V.memset(T.wz[:, 2048:4096], 0.0))
-    Y.wait_ge(S.v, v_wz)
-    load_w(range(4, 8), S.lw2)
+    vec(V.memset(T.h[:, 0:128], 0.0))
     V.wait_ge(S.gi, k_c)
     ts(T.c1[:, :], T.ic[:, :], T.fa[:, 1:2], SUB)
     ts(T.cj[:, :], T.ij[:, :], T.fa[:, 0:1], ADD)
@@ -146,75 +146,106 @@ def rank_program(g, core, T, topo):
     ts(T.r256[:, :], T.i256[:, :], 1.0, MIN)
     vec(V.memset(T.one[:, :], 1.0))
     vec(V.memset(T.tt[:, :], 0.0))
-    V.wait_ge(S.lw, 64)
-    vec(V.quantize_mx(T.cw[:, 0:512], T.pw[:, 0:512], T.wz[:, 0:2048]))
     for b in range(8):
         vec(V.memset(T.kc[:, b:b + 1], float(start_of(bitrev(b)) + 96)))
         vec(V.memset(T.wt[:, 32 * b:32 * b + 32], float(bitrev(b))))
-    V.wait_ge(S.lw2, 64)
+    V.wait_ge(S.lw, 128)
+    vec(V.quantize_mx(T.cw[:, 0:512], T.pw[:, 0:512], T.wz[:, 0:2048]))
     vec(V.quantize_mx(T.cw[:, 512:1024], T.pw[:, 512:1024], T.wz[:, 2048:4096]))
 
     V.wait_ge(S.asc, n_far * len(far) + len(near2))
     vw(n["v"])
     half = lambda t, k: t[:, 32 * k:32 * k + 32]
+    two = lambda t, k: t[:, 64 * k:64 * k + 64]
     lo, hi = me & 3, me & 1
-    vw(tt(T.m1[:, :], R(0, 4), R(4, 4), MAX))
+    v_m1 = tt(T.m1[:, :], R(0, 4), R(4, 4), MAX)
     tt(T.e1[:, :], own, R(me ^ 4), GT if me & 4 else GE)
-    k = tt(T.m2[:, :], T.m1[:, 0:64], T.m1[:, 64:128], MAX)
-    k2 = tt(T.e2[:, :], half(T.m1, lo), half(T.m1, lo ^ 2), GT if me & 2 else GE)
-    vw(k)
-    k = tt(T.e3[:, :], half(T.m2, hi), half(T.m2, hi ^ 1), GT if me & 1 else GE)
-    vw(k2)
-    vw(tt(T.e12[:, :], T.e1[:, :], T.e2[:, :], MUL))
-    vw(tt(T.e[:, :], T.e12[:, :], T.e3[:, :], MUL))
-    k = scan(T.cs[:, :], T.one[:, :], T.e[:, :], ADD, SUB)
-    k2 = tt(T.v1[:, :], T.e[:, :], T.c1[:, :], MUL)
-    vw(k)
-    k = vec(V.transpose(T.t1[:, :], T.cs[:, :]))
-    vw(k2)
-    k2 = tt(T.v3[:, :], T.v1[:, :], T.cs[:, :], ADD)
-    vw(k)
-    vw(scan(T.t2[:, :], T.r16[:, :], T.t1[:, :]))
-    vw(vec(V.transpose(T.t3[:, :], T.t2[:, :])))
-    vw(ts(T.ow[:, :], T.v3[:, :], T.t3[:, 31:32], ADD, T.cs[:, 31:32], SUB))
-    vw(vec(V.tensor_copy(T.l[:, 0:528].indirect(T.ow[:, 0:32]), T.cj[:, :])))
-    vw(tt(T.lm[:, :], T.l[:, 417:513], T.m4[:, :], MUL))
-    vw(scan(T.ls[:, :], T.r4[:, :], T.lm[:, :]))
+    vw(v_m1)
+    v_m2 = tt(T.m2[:, :], T.m1[:, 0:64], T.m1[:, 64:128], MAX)
+    v_e2 = tt(T.e2[:, :], half(T.m1, lo), half(T.m1, lo ^ 2), GT if me & 2 else GE)
+    vw(v_m2)
+    tt(T.e3[:, :], half(T.m2, hi), half(T.m2, hi ^ 1), GT if me & 1 else GE)
+    vw(v_e2)
+    v_e12 = tt(T.e12[:, :], T.e1[:, :], T.e2[:, :], MUL)
+    tt(half(T.e3b, 0), half(T.m2, 0), half(T.m2, 1), GE)
+    vw(v_e12)
+    v_e = tt(T.e[:, :], T.e12[:, :], T.e3[:, :], MUL)
+    tt(half(T.e3b, 1), half(T.m2, 1), half(T.m2, 0), GT)
+    vw(v_e)
+    v_cs = scan(T.cs[:, :], T.one[:, :], T.e[:, :], ADD, SUB)
+    v_v1 = tt(T.v1[:, :], T.e[:, :], T.c1[:, :], MUL)
+    vw(v_cs)
+    v_t1 = vec(V.transpose(T.t1[:, :], T.cs[:, :]))
+    vw(v_v1)
+    tt(T.v3[:, :], T.v1[:, :], T.cs[:, :], ADD)
+    vw(v_t1)
+    v_t2 = scan(T.t2[:, :], T.r16[:, :], T.t1[:, :])
+    v_b2 = tt(T.b2[:, :], T.m1[:, 64:128], T.m1[:, 0:64], GT)
+    vw(v_t2)
+    v_t3 = vec(V.transpose(T.t3[:, :], T.t2[:, :]))
+    vw(v_b2)
+    v_g2 = tt(T.g2[:, 64:128], T.e3b[:, :], T.b2[:, :], MUL)
+    vw(v_t3)
+    v_ow = ts(T.ow[:, :], T.v3[:, :], T.t3[:, 31:32], ADD, T.cs[:, 31:32], SUB)
+    vw(v_g2)
+    tt(T.g2[:, 0:64], T.e3b[:, :], T.g2[:, 64:128], SUB)
+    vw(v_ow)
+    v_l = vec(V.tensor_copy(T.l[:, 0:528].indirect(T.ow[:, 0:32]), T.cj[:, :]))
+    v_b1 = tt(T.b1[:, :], R(4, 4), R(0, 4), GT)
+    vw(v_l)
+    v_lm = tt(T.lm[:, :], T.l[:, 417:513], T.m4[:, :], MUL)
+    vw(v_b1)
+    v_eh = tt(T.ee[:, 128:256], T.g2[:, :], T.b1[:, :], MUL)
+    vw(v_lm)
+    v_ls = scan(T.ls[:, :], T.r4[:, :], T.lm[:, :])
+    vw(v_eh)
+    v_ee = tt(T.ee[:, 0:128], T.g2[:, :], T.ee[:, 128:256], SUB)
+    A.wait_ge(S.v, v_ee)
+    s_ep = inc("s", A.activation(T.ep[:, :], T.ee[:, :], COPY))
+    vw(v_ls)
     v_og = vec(V.tensor_copy(T.og[:, :], T.ls[:, 3:96:4]))
     A.wait_ge(S.v, v_og)
     s_h = inc("s", A.activation(T.h[:, 320:512], T.xs[:, 0:2048].indirect(T.og[:, 12:24]), COPY))
+    vw(v_ee)
+    v_cs8 = scan(T.cs8[:, :], T.r256[:, :], T.ee[:, :], MUL, SUB)
     vw(v_og)
-    vw(vec(V.tensor_copy(T.h[:, 128:320], T.xs[:, 0:2048].indirect(T.og[:, 0:12]))))
+    v_h = vec(V.tensor_copy(T.h[:, 128:320], T.xs[:, 0:2048].indirect(T.og[:, 0:12])))
+    vw(v_cs8)
+    v_tt = vec(V.tensor_copy(T.tt[:, 0:8], T.cs8[:, 31:256:32]))
+    vw(v_h)
     V.wait_ge(S.s, s_h)
     v_q = vec(V.quantize_mx(T.ca[:, 0:128], T.pa[:, 0:128], T.h[:, :]))
     g.wait_ge(S.v, v_q)
     by = lambda t, a: t[:, a:a + 96].bitcast(dt.uint8)
-    send((eng_far, S.ab, by(T.ca, 32), [(c, by(T.cb, slot(core, c))) for c in same]))
+    send((eng_far, S.ab, by(T.ca, 32), [(c, by(T.cb, slot(core, c))) for c in same]),
+         (eng_near, S.aa, by(T.ca, 32), [(mate, by(T.ca, 128))]))
     send((eng_near, S.aap, T.pa[:, 32:128], [(mate, T.pa[:, 128:224])]))
-    send((eng_near, S.aa, by(T.ca, 32), [(mate, by(T.ca, 128))]))
     g.wait_ge(S.aap, n_near)
     send((eng_far, S.abp, T.pa[:, 32:224], [(c, T.pb[:, slot(core, c):slot(core, c) + 192]) for c in same]))
     g.wait_ge(S.ab, n_far * len(same))
     on_with = [eng_far[:n_far // 2], eng_far[n_far // 2:], eng_near]
     send(*[(on_with[k], S.ac, by(T.cb, 192 * k), [(mate, by(T.cb, 192 * k + 96))]) for k in range(len(same))])
 
-    tt(half(T.e3b, 0), half(T.m2, 0), half(T.m2, 1), GE)
-    tt(half(T.e3b, 1), half(T.m2, 1), half(T.m2, 0), GT)
-    k2 = tt(T.b2[:, :], T.m1[:, 64:128], T.m1[:, 0:64], GT)
-    tt(T.b1[:, :], R(4, 4), R(0, 4), GT)
-    vw(k2)
-    vw(tt(T.g2[:, 64:128], T.e3b[:, :], T.b2[:, :], MUL))
-    vw(tt(T.g2[:, 0:64], T.e3b[:, :], T.g2[:, 64:128], SUB))
-    vw(tt(T.ee[:, 128:256], T.g2[:, :], T.b1[:, :], MUL))
-    v_ee = tt(T.ee[:, 0:128], T.g2[:, :], T.ee[:, 128:256], SUB)
-    A.wait_ge(S.v, v_ee)
-    s_ep = inc("s", A.activation(T.ep[:, :], T.ee[:, :], COPY))
-    vw(v_ee)
-    vw(scan(T.cs8[:, :], T.r256[:, :], T.ee[:, :], MUL, SUB))
-    vw(vec(V.tensor_copy(T.tt[:, 0:8], T.cs8[:, 31:256:32])))
-    k = vec(V.transpose(T.tu[:, :], T.tt[:, :]))
+    freed = [None] * 8
+
+    def product(q, bank, codes, plane, a, w, skip, at):
+        if freed[bank]:
+            P.wait_ge(S.s, freed[bank])
+        c = 512 * bank
+        k = inc("pe", P.matmul_mx(T.ps[:, c:c + w], T.cw[:, 128 * q:128 * q + 128], T.pw[:, 128 * q:128 * q + 128],
+                                  codes[:, a:a + w], plane[:, a:a + w], True, True))
+        A.wait_ge(S.pe, k)
+        freed[bank] = inc("s", A.activation(T.p[:, 768 * q + at:768 * q + at + w - skip], T.ps[:, c + skip:c + w], COPY))
+        return freed[bank]
+
+    P.wait_ge(S.v, v_q)
+    for q in range(8):
+        product(q, q, T.ca, T.pa, 0, 128, 32, 0)
+
+    vw(v_tt)
+    v_tu = vec(V.transpose(T.tu[:, :], T.tt[:, :]))
     tt(T.st1[:, :], T.kc[:, :], T.tt[:, 0:8], SUB)
-    vw(k)
+    vw(v_tu)
     vw(scan(T.tv[:, :], T.r16[:, :], T.tu[:, :]))
     vw(vec(V.transpose(T.tw[:, :], T.tv[:, :])))
     vw(tt(T.st2[:, :], T.st1[:, :], T.tw[:, 0:8], ADD))
@@ -239,46 +270,39 @@ def rank_program(g, core, T, topo):
     Y.wait_ge(S.v, tt(T.win[:, :], T.y2[:, 0:32], T.y2[:, 32:64], ADD))
     Y.dma_start(T.wn[:, :], T.win[:, :]).then_inc(S.st, 16)
 
-    freed = [None] * 8
-
-    def product(q, bank, codes, plane, a, w, at):
-        if freed[bank]:
-            P.wait_ge(S.s, freed[bank])
-        src, out = T.ps[:, 512 * bank:512 * bank + w], T.p[:, 768 * q + at:768 * q + at + w]
-        k = inc("pe", P.matmul_mx(src, T.cw[:, 128 * q:128 * q + 128], T.pw[:, 128 * q:128 * q + 128],
-                                  codes[:, a:a + w], plane[:, a:a + w], True, True))
-        A.wait_ge(S.pe, k)
-        freed[bank] = inc("s", A.activation(out, src, COPY))
-        return freed[bank]
-
-    P.wait_ge(S.v, v_q)
     P.wait_ge(S.aap, n_near)
     P.wait_ge(S.aa, n_near)
     for q in range(8):
-        product(q, q, T.ca, T.pa, 32, 192, 0)
+        product(q, q, T.ca, T.pa, 96, 128, 32, 96)
     V.wait_ge(S.it1, 128)
     V.wait_ge(S.it2, 112)
     vec(V.tensor_copy(T.off[:, 0:256:2], T.bx[:, 0:128]))
-    vec(V.tensor_copy(T.off[:, 1:256:2], T.bx[:, 128:256]))
+    v_off = vec(V.tensor_copy(T.off[:, 1:256:2], T.bx[:, 128:256]))
+    pick_of = lambda q, a, b: T.p[:, 768 * q:768 * q + 768].indirect(T.off[:, 32 * q + a // 16:32 * q + b // 16])
     P.wait_ge(S.ab, n_far * len(same))
     P.wait_ge(S.abp, n_far * len(same))
     P.wait_ge(S.ac, n_far + n_near)
     ready = []
     for q in range(8):
-        ready.append([product(q, (2 * q + k) % 8, T.cb, T.pb, 288 * k, 288, 192 + 288 * k) for k in range(2)][1])
+        ready.append([product(q, (2 * q + k) % 8, T.cb, T.pb, 288 * k, 288, 0, 192 + 288 * k) for k in range(2)][1])
+        if q == 1:
+            A.wait_ge(S.v, v_off)
+            A.wait_ge(S.s, ready[0])
+            s_half = inc("s", A.activation(T.ya[:, 256:512], pick_of(0, 256, 512), COPY))
 
-    vw(n["v"])
+    vw(v_off)
 
     def pick(q, a, b, last):
         out = T.ya[:, a:b]
-        src = T.p[:, 768 * q:768 * q + 768].indirect(T.off[:, 32 * q + a // 16:32 * q + b // 16])
         V.wait_ge(S.s, ready[q])
         if last:
             vw(last)
-        return vec(V.tensor_tensor(out, src, out, ADD) if last else V.tensor_copy(out, src))
+        return vec(V.tensor_tensor(out, pick_of(q, a, b), out, ADD) if last else V.tensor_copy(out, pick_of(q, a, b)))
 
-    last = 0
-    for q in range(6):
+    last = pick(1, 0, 256, pick(0, 0, 256, 0))
+    V.wait_ge(S.s, s_half)
+    last = pick(1, 256, 512, last)
+    for q in range(2, 6):
         last = pick(q, 0, 512, last)
     for a in (0, 256):
         k = pick(7, a, a + 256, pick(6, a, a + 256, last))

from concourse.bass import DstId, RemoteDMATransfer
from concourse.mybir import dt, AluOpType, ActivationFunctionType

F4, F, B = "float8_e4m3fn_x4", "float32", "bfloat16"
SCRATCH = {}
for _names, _w, _t in (
        ("uw", 64, B), ("xs", 2048, B), ("zt", 560, B), ("wz", 4096, B), ("h", 512, B),
        ("cz", 140, F4), ("pz", 140, "uint8"), ("cx", 512, F4), ("px", 512, "uint8"), ("cw", 1024, F4), ("pw", 1024, "uint8"),
        ("ca", 224, F4), ("pa", 224, "uint8"), ("cb", 576, F4), ("pb", 576, "uint8"),
        ("ia ib", 4, "int32"), ("fa", 4, F), ("g8 kc st1 st2", 8, F), ("v32 ms sm m1 b1 g2 x1 y1", 128, F),
        ("oz", 36, "uint16"), ("ic c1 i16 r16 one", 32, F), ("ij cj ya", 512, F), ("k4 m4 r4 lm ls", 96, F),
        ("i256 wt r ep u uv wv bx", 256, F), ("r256 ee cs8", 256, B), ("s2 m2 e3b b2 x2 y2", 64, F), ("l", 528, F),
        ("e1 e2 e3 e12 e cs t1 t2 t3 v1 v3 tt tu tv tw ix it win", 32, F),
        ("ow", 32, "uint16"), ("og", 24, "uint16"), ("off", 256, "uint16"), ("p", 6144, F)):
    for _k in _names.split():
        SCRATCH[_k] = ("sbuf", [128, _w], _t)
SCRATCH["ps"] = ("psum", [128, 4096], F)
SEMAPHORES = ["lu", "lx0", "lx1", "lx2", "lx3", "lw", "gi", "v", "s", "pe", "it1", "it2", "st",
              "asc", "aa", "aap", "ab", "abp", "ac", "loc"]

ADD, SUB, MUL, MAX, MIN = AluOpType.add, AluOpType.subtract, AluOpType.mult, AluOpType.max, AluOpType.min
GE, GT, EQ, AND = AluOpType.is_ge, AluOpType.is_gt, AluOpType.is_equal, AluOpType.bitwise_and
COPY = ActivationFunctionType.Copy


def bitrev(s):
    return (s & 1) * 4 + (s & 2) + (s >> 2)


def rank_program(g, core, T, topo):
    rank = T.rank_of(core)
    if rank is None:
        return
    S = T.sem
    V, A, P, Y = g.vector, g.scalar, g.tensor, g.sync
    n = {"v": 0, "s": 0, "pe": 0, "gi": 0, "loc": 0}

    def inc(q, call):
        n[q] += 1
        call.then_inc(S[q], 1)
        return n[q]

    vw = lambda k: V.wait_ge(S.v, k)
    vec = lambda call: inc("v", call)
    tt = lambda out, a, b, op: vec(V.tensor_tensor(out, a, b, op))
    ts = lambda out, a, s1, op, s2=None, op2=None: vec(V.tensor_scalar(out, a, s1, s2, op, op2) if op2 else V.tensor_scalar(out, a, s1, None, op))
    scan = lambda out, a, b, o0=MUL, o1=ADD: vec(V.tensor_tensor_scan(out, a, b, 0.0, o0, o1))
    iota = lambda out, pat, base, cm: inc("gi", g.iota(out, pat, base, cm, allow_small_or_imprecise_dtypes=True))

    cores = list(T.cores)
    chips = []
    for c in cores:
        if topo.chip(c) not in chips:
            chips.append(topo.chip(c))
    on = lambda ch: [c for c in cores if topo.chip(c) == ch]
    mychip = topo.chip(core)
    kind = on(mychip).index(core)
    mate = [c for c in on(mychip) if c != core][0]
    far = [c for c in cores if topo.chip(c) != mychip]
    same = [on(ch)[kind] for ch in chips if ch != mychip]
    slot = lambda frm, to: 192 * [ch for ch in chips if ch != topo.chip(to)].index(topo.chip(frm))
    eng_far = [e for e in topo.engines(core, mate) if all(e in topo.engines(core, c) for c in far)]
    eng_near = [e for e in topo.engines(core, mate) if e not in eng_far][:4]
    n_far, n_near = len(eng_far), len(eng_near)
    did = lambda c: DstId(rid=topo.addr(c)[0], pnc=topo.addr(c)[1])

    def start_of(s):
        c = cores[s]
        if c in (core, mate):
            return 0 if c == core else 96
        return 192 + slot(c, core) + (0 if c in same else 96)

    def send(*transfers):
        n["loc"] += sum(len(m) for m, _, _, _ in transfers)
        g.remote_dma_fused([RemoteDMATransfer(dst_ids=[did(c) for c, _ in to], dma_engine_mask=sum(1 << e for e in m), remote_sem=sem,
                                              srcs=[src], dsts=[d for _, d in to], alu_op=0) for m, sem, src, to in transfers], local_sem=S.loc)

    Y.dma_start(T.uw[:, 0:64], T.us[:, 0:64]).then_inc(S.lu, 16)
    for q, k in ((A, 0), (Y, 1), (A, 2), (Y, 3)):
        q.dma_start(T.xs[:, 512 * k:512 * k + 512], T.x[:, 512 * k:512 * k + 512]).then_inc(S["lx%d" % k], 16)

    inc("gi", g.iota(T.ia[:, 0:1], [[0, 1]], 0, 1))
    inc("gi", g.iota(T.ia[:, 1:2], [[0, 1]], 0, 32))
    k_a = iota(T.g8[:, :], [[4, 8]], 0, 0)
    k_b = iota(T.v32[:, :], [[1, 4], [0, 32]], 0, 0)
    iota(T.ic[:, :], [[-1, 32]], 512, 0)
    iota(T.k4[:, :], [[0, 24], [1, 4]], 0, 0)
    iota(T.i16[:, :], [[0, 2], [1, 16]], 0, 0)
    iota(T.ij[:, :], [[4, 32], [128, 16]], 0, 0)
    k_c = iota(T.i256[:, :], [[0, 8], [1, 32]], 0, 0)

    vec(V.memset(T.oz[:, :], 32))
    v_z = vec(V.memset(T.wz[:, 0:1024], 0.0))
    A.wait_ge(S.v, v_z)
    s_wz = inc("s", A.activation(T.wz[:, 3072:4096], T.wz[:, 0:1024], COPY))
    V.wait_ge(S.gi, k_a)
    ts(T.ib[:, 0:1], T.ia[:, 0:1], 3, AND)
    ts(T.ib[:, 1:2], T.ia[:, 1:2], 511, AND)
    vw(ts(T.ib[:, 2:3], T.ia[:, 0:1], 12, AND, 2, AluOpType.arith_shift_right))
    vw(vec(V.tensor_copy(T.fa[:, 0:3], T.ib[:, 0:3])))
    v_oz = ts(T.oz[:, 3:32:4], T.g8[:, :], T.fa[:, 0:1], ADD)
    vec(V.memset(T.wz[:, 1024:2048], 0.0))
    V.wait_ge(S.gi, k_b)
    ts(T.ms[:, :], T.v32[:, :], T.fa[:, 0:1], EQ)

    A.wait_ge(S.lu, 16)
    A.wait_ge(S.v, v_oz)
    s_zt = inc("s", A.activation(T.zt[:, :], T.uw[:, 0:64].indirect(T.oz[:, 0:35]), COPY))

    for q in range(4):
        if q == 3:
            V.wait_ge(S.s, s_zt)
            vec(V.quantize_mx(T.cz[:, :], T.pz[:, :], T.zt[:, :]))
        V.wait_ge(S["lx%d" % q], 16)
        v_x = vec(V.quantize_mx(T.cx[:, 128 * q:128 * q + 128], T.px[:, 128 * q:128 * q + 128], T.xs[:, 512 * q:512 * q + 512]))
        if q == 0:
            v_wz = vec(V.memset(T.wz[:, 2048:3072], 0.0))
    for q in range(4):
        a, b = 12 - 4 * q, 128 * q
        P.wait_ge(S.v, v_x if q == 3 else v_x - 1)
        k_sc = inc("pe", P.matmul_mx(T.ps[:, 3584:3712], T.cz[:, a:a + 128], T.pz[:, a:a + 128],
                                     T.cx[:, b:b + 128], T.px[:, b:b + 128], q == 0, q == 3))

    Y.wait_ge(S.v, v_wz)
    Y.wait_ge(S.s, s_wz)
    for q in range(8):
        Y.dma_start(T.wz[16 * q:16 * q + 16, 512 * q:512 * q + 512], T.w[16 * q:16 * q + 16, :]).then_inc(S.lw, 16)

    V.wait_ge(S.pe, k_sc)
    me = bitrev(rank)
    R = lambda b, q=1: T.r[:, 32 * b:32 * (b + q)]
    own = R(me)
    vw(tt(T.sm[:, :], T.ps[:, 3584:3712], T.ms[:, :], MUL))
    vw(tt(T.s2[:, :], T.sm[:, 0:64], T.sm[:, 64:128], ADD))
    g.wait_ge(S.v, tt(own, T.s2[:, 0:32], T.s2[:, 32:64], ADD))
    near2 = eng_near[:2]
    send((eng_far, S.asc, own, [(c, own) for c in far]), (near2, S.asc, own, [(mate, own)]))

    vec(V.memset(T.h[:, 0:128], 0.0))
    V.wait_ge(S.gi, k_c)
    ts(T.c1[:, :], T.ic[:, :], T.fa[:, 1:2], SUB)
    ts(T.cj[:, :], T.ij[:, :], T.fa[:, 0:1], ADD)
    ts(T.m4[:, :], T.k4[:, :], T.fa[:, 2:3], EQ)
    ts(T.r4[:, :], T.k4[:, :], 1.0, MIN)
    ts(T.r16[:, :], T.i16[:, :], 1.0, MIN)
    ts(T.r256[:, :], T.i256[:, :], 1.0, MIN)
    vec(V.memset(T.one[:, :], 1.0))
    vec(V.memset(T.tt[:, :], 0.0))
    for b in range(8):
        vec(V.memset(T.kc[:, b:b + 1], float(start_of(bitrev(b)) + 96)))
        vec(V.memset(T.wt[:, 32 * b:32 * b + 32], float(bitrev(b))))
    V.wait_ge(S.lw, 128)
    vec(V.quantize_mx(T.cw[:, 0:512], T.pw[:, 0:512], T.wz[:, 0:2048]))
    vec(V.quantize_mx(T.cw[:, 512:1024], T.pw[:, 512:1024], T.wz[:, 2048:4096]))

    V.wait_ge(S.asc, n_far * len(far) + len(near2))
    vw(n["v"])
    half = lambda t, k: t[:, 32 * k:32 * k + 32]
    two = lambda t, k: t[:, 64 * k:64 * k + 64]
    lo, hi = me & 3, me & 1
    v_m1 = tt(T.m1[:, :], R(0, 4), R(4, 4), MAX)
    tt(T.e1[:, :], own, R(me ^ 4), GT if me & 4 else GE)
    vw(v_m1)
    v_m2 = tt(T.m2[:, :], T.m1[:, 0:64], T.m1[:, 64:128], MAX)
    v_e2 = tt(T.e2[:, :], half(T.m1, lo), half(T.m1, lo ^ 2), GT if me & 2 else GE)
    vw(v_m2)
    tt(T.e3[:, :], half(T.m2, hi), half(T.m2, hi ^ 1), GT if me & 1 else GE)
    vw(v_e2)
    v_e12 = tt(T.e12[:, :], T.e1[:, :], T.e2[:, :], MUL)
    tt(half(T.e3b, 0), half(T.m2, 0), half(T.m2, 1), GE)
    vw(v_e12)
    v_e = tt(T.e[:, :], T.e12[:, :], T.e3[:, :], MUL)
    tt(half(T.e3b, 1), half(T.m2, 1), half(T.m2, 0), GT)
    vw(v_e)
    v_cs = scan(T.cs[:, :], T.one[:, :], T.e[:, :], ADD, SUB)
    v_v1 = tt(T.v1[:, :], T.e[:, :], T.c1[:, :], MUL)
    vw(v_cs)
    v_t1 = vec(V.transpose(T.t1[:, :], T.cs[:, :]))
    vw(v_v1)
    tt(T.v3[:, :], T.v1[:, :], T.cs[:, :], ADD)
    vw(v_t1)
    v_t2 = scan(T.t2[:, :], T.r16[:, :], T.t1[:, :])
    v_b2 = tt(T.b2[:, :], T.m1[:, 64:128], T.m1[:, 0:64], GT)
    vw(v_t2)
    v_t3 = vec(V.transpose(T.t3[:, :], T.t2[:, :]))
    vw(v_b2)
    v_g2 = tt(T.g2[:, 64:128], T.e3b[:, :], T.b2[:, :], MUL)
    vw(v_t3)
    v_ow = ts(T.ow[:, :], T.v3[:, :], T.t3[:, 31:32], ADD, T.cs[:, 31:32], SUB)
    vw(v_g2)
    tt(T.g2[:, 0:64], T.e3b[:, :], T.g2[:, 64:128], SUB)
    vw(v_ow)
    v_l = vec(V.tensor_copy(T.l[:, 0:528].indirect(T.ow[:, 0:32]), T.cj[:, :]))
    v_b1 = tt(T.b1[:, :], R(4, 4), R(0, 4), GT)
    vw(v_l)
    v_lm = tt(T.lm[:, :], T.l[:, 417:513], T.m4[:, :], MUL)
    vw(v_b1)
    v_eh = tt(T.ee[:, 128:256], T.g2[:, :], T.b1[:, :], MUL)
    vw(v_lm)
    v_ls = scan(T.ls[:, :], T.r4[:, :], T.lm[:, :])
    vw(v_eh)
    v_ee = tt(T.ee[:, 0:128], T.g2[:, :], T.ee[:, 128:256], SUB)
    A.wait_ge(S.v, v_ee)
    s_ep = inc("s", A.activation(T.ep[:, :], T.ee[:, :], COPY))
    vw(v_ls)
    v_og = vec(V.tensor_copy(T.og[:, :], T.ls[:, 3:96:4]))
    A.wait_ge(S.v, v_og)
    s_h = inc("s", A.activation(T.h[:, 320:512], T.xs[:, 0:2048].indirect(T.og[:, 12:24]), COPY))
    vw(v_ee)
    v_cs8 = scan(T.cs8[:, :], T.r256[:, :], T.ee[:, :], MUL, SUB)
    vw(v_og)
    v_h = vec(V.tensor_copy(T.h[:, 128:320], T.xs[:, 0:2048].indirect(T.og[:, 0:12])))
    vw(v_cs8)
    v_tt = vec(V.tensor_copy(T.tt[:, 0:8], T.cs8[:, 31:256:32]))
    vw(v_h)
    V.wait_ge(S.s, s_h)
    v_q = vec(V.quantize_mx(T.ca[:, 0:128], T.pa[:, 0:128], T.h[:, :]))
    g.wait_ge(S.v, v_q)
    by = lambda t, a: t[:, a:a + 96].bitcast(dt.uint8)
    send((eng_far, S.ab, by(T.ca, 32), [(c, by(T.cb, slot(core, c))) for c in same]),
         (eng_near, S.aa, by(T.ca, 32), [(mate, by(T.ca, 128))]))
    send((eng_near, S.aap, T.pa[:, 32:128], [(mate, T.pa[:, 128:224])]))
    g.wait_ge(S.aap, n_near)
    send((eng_far, S.abp, T.pa[:, 32:224], [(c, T.pb[:, slot(core, c):slot(core, c) + 192]) for c in same]))
    g.wait_ge(S.ab, n_far * len(same))
    on_with = [eng_far[:n_far // 2], eng_far[n_far // 2:], eng_near]
    send(*[(on_with[k], S.ac, by(T.cb, 192 * k), [(mate, by(T.cb, 192 * k + 96))]) for k in range(len(same))])

    freed = [None] * 8

    def product(q, bank, codes, plane, a, w, skip, at):
        if freed[bank]:
            P.wait_ge(S.s, freed[bank])
        c = 512 * bank
        k = inc("pe", P.matmul_mx(T.ps[:, c:c + w], T.cw[:, 128 * q:128 * q + 128], T.pw[:, 128 * q:128 * q + 128],
                                  codes[:, a:a + w], plane[:, a:a + w], True, True))
        A.wait_ge(S.pe, k)
        freed[bank] = inc("s", A.activation(T.p[:, 768 * q + at:768 * q + at + w - skip], T.ps[:, c + skip:c + w], COPY))
        return freed[bank]

    P.wait_ge(S.v, v_q)
    for q in range(8):
        product(q, q, T.ca, T.pa, 0, 128, 32, 0)

    vw(v_tt)
    v_tu = vec(V.transpose(T.tu[:, :], T.tt[:, :]))
    tt(T.st1[:, :], T.kc[:, :], T.tt[:, 0:8], SUB)
    vw(v_tu)
    vw(scan(T.tv[:, :], T.r16[:, :], T.tu[:, :]))
    vw(vec(V.transpose(T.tw[:, :], T.tv[:, :])))
    vw(tt(T.st2[:, :], T.st1[:, :], T.tw[:, 0:8], ADD))
    V.wait_ge(S.s, s_ep)
    vw(tt(T.ep[:, 0:256:32], T.ep[:, 0:256:32], T.st2[:, :], SUB))
    vw(scan(T.u[:, :], T.r256[:, :], T.ep[:, :], MUL, SUB))
    vw(tt(T.uv[:, :], T.u[:, :], T.ee[:, :], MUL))
    vw(tt(T.x1[:, :], T.uv[:, 0:128], T.uv[:, 128:256], ADD))
    vw(tt(T.x2[:, :], T.x1[:, 0:64], T.x1[:, 64:128], ADD))
    vw(tt(T.ix[:, :], T.x2[:, 0:32], T.x2[:, 32:64], ADD))
    v_it = vec(V.transpose(T.it[:, :], T.ix[:, :]))
    for q, b in ((Y, 0), (A, 1)):
        q.wait_ge(S.v, v_it)
        for k in range(4):
            q.dma_start(T.bx[0:16, 128 * b + 32 * k:128 * b + 32 * k + 32], T.it[32 * k + 16 * b:32 * k + 16 * b + 16, :]).then_inc(S.it1, 16)
    Y.wait_ge(S.it1, 128)
    for q in range(1, 8):
        Y.dma_start(T.bx[16 * q:16 * q + 16, :], T.bx[0:16, :]).then_inc(S.it2, 16)
    vw(tt(T.wv[:, :], T.ee[:, :], T.wt[:, :], MUL))
    vw(tt(T.y1[:, :], T.wv[:, 0:128], T.wv[:, 128:256], ADD))
    vw(tt(T.y2[:, :], T.y1[:, 0:64], T.y1[:, 64:128], ADD))
    Y.wait_ge(S.v, tt(T.win[:, :], T.y2[:, 0:32], T.y2[:, 32:64], ADD))
    Y.dma_start(T.wn[:, :], T.win[:, :]).then_inc(S.st, 16)

    P.wait_ge(S.aap, n_near)
    P.wait_ge(S.aa, n_near)
    for q in range(8):
        product(q, q, T.ca, T.pa, 96, 128, 32, 96)
    V.wait_ge(S.it1, 128)
    V.wait_ge(S.it2, 112)
    vec(V.tensor_copy(T.off[:, 0:256:2], T.bx[:, 0:128]))
    v_off = vec(V.tensor_copy(T.off[:, 1:256:2], T.bx[:, 128:256]))
    pick_of = lambda q, a, b: T.p[:, 768 * q:768 * q + 768].indirect(T.off[:, 32 * q + a // 16:32 * q + b // 16])
    P.wait_ge(S.ab, n_far * len(same))
    P.wait_ge(S.abp, n_far * len(same))
    P.wait_ge(S.ac, n_far + n_near)
    ready = []
    for q in range(8):
        ready.append([product(q, (2 * q + k) % 8, T.cb, T.pb, 288 * k, 288, 0, 192 + 288 * k) for k in range(2)][1])
        if q == 1:
            A.wait_ge(S.v, v_off)
            A.wait_ge(S.s, ready[0])
            s_half = inc("s", A.activation(T.ya[:, 256:512], pick_of(0, 256, 512), COPY))

    vw(v_off)

    def pick(q, a, b, last):
        out = T.ya[:, a:b]
        V.wait_ge(S.s, ready[q])
        if last:
            vw(last)
        return vec(V.tensor_tensor(out, pick_of(q, a, b), out, ADD) if last else V.tensor_copy(out, pick_of(q, a, b)))

    last = pick(1, 0, 256, pick(0, 0, 256, 0))
    V.wait_ge(S.s, s_half)
    last = pick(1, 256, 512, last)
    for q in range(2, 6):
        last = pick(q, 0, 512, last)
    for a in (0, 256):
        k = pick(7, a, a + 256, pick(6, a, a + 256, last))
        Y.wait_ge(S.v, k)
        Y.dma_start(T.y[:, a:a + 256], T.ya[:, a:a + 256]).then_inc(S.st, 16)
    Y.wait_ge(S.st, 48)
    g.wait_ge(S.loc, n["loc"])
    g.wait_ge(S.v, n["v"])
    g.wait_ge(S.s, n["s"])
    g.wait_ge(S.pe, n["pe"])
